import numpy as np
import ml_dtypes


def mxq(x, axis, fmt="e4m3"):
    dtype, down = {"e4m3": (ml_dtypes.float8_e4m3fn, 7), "e5m2": (ml_dtypes.float8_e5m2, 14)}[fmt]
    v = np.moveaxis(np.asarray(x, np.float32).astype(ml_dtypes.bfloat16).astype(np.float64), axis, -1)
    blocks = v.reshape(v.shape[:-1] + (-1, 32))
    amax = np.abs(blocks).max(-1, keepdims=True)
    byte = np.maximum(np.where(amax > 0, np.frexp(amax)[1] - 1 + 127, 0) - down, 1)
    scale = np.exp2(byte - 127.0)
    codes = (blocks / scale).astype(np.float32).astype(dtype).astype(np.float64)
    return np.moveaxis((codes * scale).reshape(v.shape), -1, axis)


WIDE = False


def mx_kscale(k):
    if not WIDE:
        return np.ones(k)
    levels = np.array([24, -24, 12, -12, 0])
    if k % 512:
        return np.exp2(np.random.permutation(np.resize(levels, k // 32))).repeat(32)
    a = np.empty((k // 512, 16))
    for p in range(k // 512):
        a[p, :8] = np.random.permutation(np.resize(levels, 8))
        for g in range(8):
            far = levels[np.abs(levels - a[p, g]) >= 10]
            a[p, g + 8] = far[np.random.randint(len(far))]
    return np.exp2(a.ravel()).repeat(32)


def f64(x):
    return np.asarray(x).astype(np.float64)


def striped(idx):
    return np.tile(idx.reshape(-1, 16).T, (8, 1)).astype(np.uint16)


def unstriped(offs):
    return offs[:16].T.reshape(-1).astype(np.int64)


E2M1 = np.array([0.0, 0.5, 1.0, 1.5, 2.0, 3.0, 4.0, 6.0, -0.0, -0.5, -1.0, -1.5, -2.0, -3.0, -4.0, -6.0])


def pack_weight(w, fmt):
    k, n = w.shape
    w = f64(np.asarray(w, np.float32).astype(ml_dtypes.bfloat16)).reshape(k // 32, 32, n)
    amax = np.abs(w).max(1)
    if fmt == "e4m3":
        byte = np.frexp(amax)[1] - 1 + 127 - 7
    else:
        mant, ex = np.frexp(amax / 6.0)
        byte = np.where(mant > 0.5, ex, ex - 1) + 127
    byte = np.clip(np.where(amax > 0, byte, 1), 1, 254)
    scaled = (w * np.exp2(127.0 - byte)[:, None, :]).reshape(k, n).astype(np.float32)
    by_word = np.ascontiguousarray(scaled.reshape(k // 512, 128, 4, n).transpose(0, 1, 3, 2))
    if fmt == "e4m3":
        words = by_word.astype(ml_dtypes.float8_e4m3fn).view(np.uint8)
    else:
        c = by_word.astype(ml_dtypes.float4_e2m1fn).view(np.uint8) & 0xF
        words = (c[..., 0::2] | (c[..., 1::2] << 4)).reshape(k // 512, 128, 2 * n)
    return np.ascontiguousarray(words), np.ascontiguousarray(byte.astype(np.uint8).reshape(k // 512, 16, n))


def unpack_weight(words, scales, fmt):
    g, _, n = scales.shape
    words = np.ascontiguousarray(words).reshape(g, 128, n, -1)
    if fmt == "e4m3":
        vals = words.view(ml_dtypes.float8_e4m3fn).astype(np.float64)
    else:
        nib = np.empty((g, 128, n, 4), np.uint8)
        nib[..., 0::2] = words & 0xF
        nib[..., 1::2] = words >> 4
        vals = E2M1[nib]
    vals = vals * np.repeat(np.exp2(scales.astype(np.float64) - 127.0), 8, axis=1)[..., None]
    return vals.transpose(0, 1, 3, 2).reshape(g * 512, n)


def pack_table4(v):
    words, scales = pack_weight(v, "e2m1")
    g, t = words.shape[0] // 2, v.shape[1]
    return np.ascontiguousarray(words.reshape(g, 2, 128, t, 2).transpose(0, 2, 3, 1, 4).reshape(g, 128, t, 4)), scales


def unpack_table4(words, scales):
    g, _, t, _ = words.shape
    return unpack_weight(words.reshape(g, 128, t, 2, 2).transpose(0, 3, 1, 2, 4).reshape(2 * g, 128, 2 * t), scales, "e2m1")


K, R, N, T, J = 1024, 512, 512, 4096, 1024


def setup_inputs():
    n = np.random.standard_normal
    s = mx_kscale(K)[:, None]
    u = mx_kscale(R)[:, None]
    p_tab = pack_table4(n((K, T)) * s)
    p_wb = pack_weight(0.7 * n((K, N)) / np.sqrt(K) / s, "e2m1")
    p_dn = pack_weight(n((K, R)) / np.sqrt(K) / s * u.T, "e2m1")
    return {
        "tab_words": p_tab[0],
        "tab_scales": p_tab[1],
        "wb_words": p_wb[0],
        "wb_scales": p_wb[1],
        "dn_words": p_dn[0],
        "dn_scales": p_dn[1],
        "upw": (2.0 * n((R, N)) / np.sqrt(R) / u).astype(np.float32),
        "x0T": (n((N, T))).astype(np.float32),
        "b": (0.3 * n(N)).astype(np.float32),
        "offs": striped(np.random.permutation(T)[:J]),
    }


def reference(tab_words, tab_scales, wb_words, wb_scales, dn_words, dn_scales, upw, x0T, b, offs):
    idx = unstriped(offs)
    tab_ = unpack_table4(tab_words, tab_scales)[:, idx]
    wb_ = unpack_weight(wb_words, wb_scales, "e2m1")
    dn_ = unpack_weight(dn_words, dn_scales, "e2m1")
    hs = dn_.T @ tab_
    h = np.maximum(hs, 0.0)
    h_ = mxq(h, 0, "e4m3")
    upw_ = mxq(f64(upw), 0, "e4m3")
    y = wb_.T @ tab_ + upw_.T @ h_
    return f64(x0T)[:, idx] * (y + f64(b)[:, None]) + f64(x0T)[:, idx]

@@ -1,0 +1,161 @@
+from contextlib import ExitStack
+
+import concourse.mybir as mybir
+
+K, R, N, T, J = 1024, 512, 512, 4096, 1024
+FLOPS = 2 * J * (K * R + K * N + R * N)
+
+F32 = mybir.dt.float32
+BF16 = mybir.dt.bfloat16
+I32 = mybir.dt.int32
+U32 = mybir.dt.uint32
+U16 = mybir.dt.uint16
+U8 = mybir.dt.uint8
+FP8X4 = mybir.dt.float8_e4m3fn_x4
+FP4X4 = mybir.dt.float4_e2m1fn_x4
+ACT = mybir.ActivationFunctionType
+ALU = mybir.AluOpType
+
+P = 128
+PASSES = 2
+HALF = 512
+HALVES = J // HALF
+CH = 128
+NT = N // P
+DN0 = J
+WB0 = J + R
+PLANE = J + R + N
+
+
+def tile_list_xcross_relu_kernel(tc, tab_words, tab_scales, wb_words, wb_scales, dn_words, dn_scales, upw, x0T, b, offs, out):
+    nc = tc.nc
+    with ExitStack() as ctx:
+        keep = ctx.enter_context(tc.tile_pool(name="keep", bufs=1))
+        ps_h = ctx.enter_context(tc.psum_pool(name="ps_h", bufs=3))
+        ps_y = ctx.enter_context(tc.psum_pool(name="ps_y", bufs=5))
+
+        offsets = keep.tile([P, J // 16], U16, name="offsets")
+        nc.sync.dma_start(offsets[:], offs)
+
+        tab_sc = keep.tile([P, T // 4], I32, name="tab_sc", align_bytes=64)
+        planes = keep.tile([P, PASSES, PLANE // 4], I32, name="planes", align_bytes=64)
+        nc.vector.memset(tab_sc[32:64, :], 0)
+        nc.vector.memset(tab_sc[64:128, :], 0)
+        nc.vector.memset(planes[:], 0)
+        g_sc = keep.tile([P, J], U8, name="g_sc", align_bytes=64)
+        dn_w = keep.tile([P, PASSES, 2 * R], U8, name="dn_w", align_bytes=64)
+        tab_w = keep.tile([P, T], I32, name="tab_w", align_bytes=64)
+        wb_w = keep.tile([P, PASSES, N // 2], I32, name="wb_w", align_bytes=64)
+        up_raw = keep.tile([P, 4, N], F32, name="up_raw")
+        b_raw = keep.tile([P, NT], F32, name="b_raw")
+        b1 = keep.tile([P, NT], F32, name="b1")
+        x0 = [keep.tile([P, T], F32, name="x0_0")]
+
+        def scale_rows(scales):
+            return scales.rearrange("a q n -> q a n").bitcast(I32)
+
+        with tc.tile_pool(name="stage", bufs=1) as stage:
+            rows = stage.tile([P, PLANE // 4], I32, name="rows", align_bytes=64)
+            dn_sc_raw = stage.tile([P, R // 4], I32, name="dn_sc_raw", align_bytes=64)
+            nc.vector.memset(dn_sc_raw[32:64, :], 0)
+            nc.vector.memset(dn_sc_raw[64:128, :], 0)
+            dn_raw = stage.tile([P, PASSES, R // 2], I32, name="dn_raw", align_bytes=64)
+            nc.sync.dma_start(out=tab_sc[0:32, :], in_=scale_rows(tab_scales))
+            nc.sync.dma_start(out=dn_sc_raw[0:32, :], in_=scale_rows(dn_scales))
+            nc.sync.dma_start(out=rows[0:32, WB0 // 4 : (WB0 + N) // 4], in_=scale_rows(wb_scales))
+            nc.sync.dma_start(out=dn_raw[:], in_=dn_words.rearrange("a p w -> p a w").bitcast(I32))
+            nc.sync.dma_start(out=tab_w[:], in_=tab_words[0].rearrange("p t c -> p (t c)").bitcast(I32))
+            nc.sync.dma_start(out=wb_w[:], in_=wb_words.rearrange("a p w -> p a w").bitcast(I32))
+            nc.sync.dma_start(out=up_raw[:], in_=upw.rearrange("(p t) n -> p t n", t=4))
+            nc.sync.dma_start(out=x0[0][:], in_=x0T[0:P, :])
+            with nc.allow_non_contiguous_dma(reason="one bias value a partition"):
+                nc.gpsimd.dma_start(out=b_raw[:], in_=b.rearrange("(c p) -> p c", p=P))
+            nc.gpsimd.tensor_scalar(out=b1[:], in0=b_raw[:], scalar1=1.0, scalar2=None, op0=ALU.add)
+
+            nc.vector.tensor_copy(out=g_sc[:], in_=tab_sc[:].bitcast(U8).indirect(offsets[:]))
+            nc.vector.tensor_copy(
+                out=rows[:].bitcast(U8)[:, DN0 : DN0 + R].rearrange("p (t m) -> p t m", t=4),
+                in_=dn_sc_raw[:].bitcast(U8).rearrange("p (m t) -> p t m", t=4),
+            )
+            nc.vector.tensor_copy(out=rows[0:32, 0 : J // 4], in_=g_sc[0:32, :].bitcast(I32))
+            for q in range(4):
+                nc.scalar.dma_start(out=planes[32 * q : 32 * q + 4, :, :], in_=rows[8 * q : 8 * q + 8, :])
+            nc.vector.tensor_copy(
+                out=dn_w[:].bitcast(U16).rearrange("p a (t m) -> p a t m", t=4),
+                in_=dn_raw[:].bitcast(U16).rearrange("p a (m t) -> p a t m", t=4),
+            )
+
+        late = ctx.enter_context(tc.tile_pool(name="late", bufs=1))
+        for c in range(1, NT):
+            x0c = late.tile([P, T], F32, name="x0_%d" % c)
+            nc.sync.dma_start(out=x0c[:], in_=x0T[c * P : (c + 1) * P, :])
+            x0.append(x0c)
+
+        def offs_of(j0, n):
+            return offsets[:, j0 // 16 : (j0 + n) // 16]
+
+        def plane(a, c0, n):
+            return planes[:, a, :].bitcast(U8)[:, c0 : c0 + n]
+
+        g_w = [keep.tile([P, HALF], U32, name="g_w_%d" % h, align_bytes=64) for h in range(HALVES)]
+        t_w = [keep.tile([P, PASSES, 2 * HALF], U8, name="t_w_%d" % h, align_bytes=64) for h in range(HALVES)]
+        for h in range(HALVES):
+            nc.vector.tensor_copy(out=g_w[h][:], in_=tab_w[:].bitcast(U32).indirect(offs_of(h * HALF, HALF)))
+            nc.vector.tensor_copy(
+                out=t_w[h][:].bitcast(U16),
+                in_=g_w[h][:].bitcast(U16).rearrange("p (j d) -> p d j", d=PASSES),
+            )
+
+        up_bf = keep.tile([P, N, 4], BF16, name="up_bf", align_bytes=64)
+        up_w = keep.tile([P, N], U32, name="up_w", align_bytes=64)
+        up_sc = keep.tile([P, N], U8, name="up_sc", align_bytes=64)
+        nc.vector.tensor_copy(out=up_bf[:], in_=up_raw[:].rearrange("p t n -> p n t"))
+        nc.vector.quantize_mx(out=up_w[:].bitcast(FP8X4), scales=up_sc[:], in_=up_bf[:].rearrange("p n t -> p (n t)"))
+
+        h_bf = [keep.tile([P, HALF, 4], BF16, name="h_bf_%d" % h, align_bytes=64) for h in range(HALVES)]
+        h_w = [keep.tile([P, HALF], U32, name="h_w_%d" % h, align_bytes=64) for h in range(HALVES)]
+        h_sc = [keep.tile([P, HALF], U8, name="h_sc_%d" % h, align_bytes=64) for h in range(HALVES)]
+        for h in range(HALVES):
+            for j0 in range(0, HALF, CH):
+                hs = ps_h.tile([P, 4, CH], F32, name="hs")
+                for t in range(4):
+                    for a in range(PASSES):
+                        nc.tensor.matmul_mx(
+                            out=hs[:, t, :],
+                            lhsT=dn_w[:, a, 2 * P * t : 2 * P * (t + 1)].bitcast(FP4X4),
+                            lhsT_scale=plane(a, DN0 + P * t, P),
+                            rhs=t_w[h][:, a, 2 * j0 : 2 * (j0 + CH)].bitcast(FP4X4),
+                            rhs_scale=plane(a, h * HALF + j0, CH),
+                            start=(a == 0),
+                            stop=(a == PASSES - 1),
+                        )
+                nc.scalar.activation(out=h_bf[h][:, j0 : j0 + CH, :], in_=hs[:].rearrange("p t n -> p n t"), func=ACT.Relu)
+            nc.vector.quantize_mx(out=h_w[h][:].bitcast(FP8X4), scales=h_sc[h][:], in_=h_bf[h][:].rearrange("p j t -> p (j t)"))
+
+        for c in range(NT):
+            for h in range(HALVES):
+                y = ps_y.tile([P, HALF], F32, name="y")
+                for a in range(PASSES):
+                    nc.tensor.matmul_mx(
+                        out=y[:],
+                        lhsT=wb_w[:, a, :].bitcast(U8)[:, 2 * P * c : 2 * P * (c + 1)].bitcast(FP4X4),
+                        lhsT_scale=plane(a, WB0 + P * c, P),
+                        rhs=t_w[h][:, a, :].bitcast(FP4X4),
+                        rhs_scale=plane(a, h * HALF, HALF),
+                        start=(a == 0),
+                        stop=False,
+                    )
+                nc.tensor.matmul_mx(
+                    out=y[:],
+                    lhsT=up_w[:, P * c : P * (c + 1)].bitcast(FP8X4),
+                    lhsT_scale=up_sc[:, P * c : P * (c + 1)],
+                    rhs=h_w[h][:].bitcast(FP8X4),
+                    rhs_scale=h_sc[h][:],
+                    start=False,
+                    stop=True,
+                )
+                yb = keep.tile([P, HALF], F32, name="yb_%d_%d" % (c, h))
+                nc.scalar.activation(out=yb[:], in_=y[:], func=ACT.Identity, bias=b1[:, c : c + 1])
+                res = keep.tile([P, HALF], F32, name="res_%d_%d" % (c, h))
+                nc.vector.tensor_tensor(out=res[:], in0=x0[c][:].indirect(offs_of(h * HALF, HALF)), in1=yb[:], op=ALU.mult)
+                nc.sync.dma_start(out=out[c * P : (c + 1) * P, h * HALF : (h + 1) * HALF], in_=res[:])

@@ -25,6 +25,7 @@ NT = N // P
 DN0 = J
 WB0 = J + R
 PLANE = J + R + N
+LAST_PIECES = [512, 256, 256]
 
 
 def tile_list_xcross_relu_kernel(tc, tab_words, tab_scales, wb_words, wb_scales, dn_words, dn_scales, upw, x0T, b, offs, out):
@@ -46,20 +47,19 @@ def tile_list_xcross_relu_kernel(tc, tab_words, tab_scales, wb_words, wb_scales,
         dn_w = keep.tile([P, PASSES, 2 * R], U8, name="dn_w", align_bytes=64)
         tab_w = keep.tile([P, T], I32, name="tab_w", align_bytes=64)
         wb_w = keep.tile([P, PASSES, N // 2], I32, name="wb_w", align_bytes=64)
+        rows = keep.tile([P, PLANE // 4], I32, name="rows", align_bytes=64)
+        dn_raw = keep.tile([P, PASSES, R // 2], I32, name="dn_raw", align_bytes=64)
         up_raw = keep.tile([P, 4, N], F32, name="up_raw")
         b_raw = keep.tile([P, NT], F32, name="b_raw")
         b1 = keep.tile([P, NT], F32, name="b1")
-        x0 = [keep.tile([P, T], F32, name="x0_0")]
 
         def scale_rows(scales):
             return scales.rearrange("a q n -> q a n").bitcast(I32)
 
         with tc.tile_pool(name="stage", bufs=1) as stage:
-            rows = stage.tile([P, PLANE // 4], I32, name="rows", align_bytes=64)
             dn_sc_raw = stage.tile([P, R // 4], I32, name="dn_sc_raw", align_bytes=64)
             nc.vector.memset(dn_sc_raw[32:64, :], 0)
             nc.vector.memset(dn_sc_raw[64:128, :], 0)
-            dn_raw = stage.tile([P, PASSES, R // 2], I32, name="dn_raw", align_bytes=64)
             nc.sync.dma_start(out=tab_sc[0:32, :], in_=scale_rows(tab_scales))
             nc.sync.dma_start(out=dn_sc_raw[0:32, :], in_=scale_rows(dn_scales))
             nc.sync.dma_start(out=rows[0:32, WB0 // 4 : (WB0 + N) // 4], in_=scale_rows(wb_scales))
@@ -67,26 +67,27 @@ def tile_list_xcross_relu_kernel(tc, tab_words, tab_scales, wb_words, wb_scales,
             nc.sync.dma_start(out=tab_w[:], in_=tab_words[0].rearrange("p t c -> p (t c)").bitcast(I32))
             nc.sync.dma_start(out=wb_w[:], in_=wb_words.rearrange("a p w -> p a w").bitcast(I32))
             nc.sync.dma_start(out=up_raw[:], in_=upw.rearrange("(p t) n -> p t n", t=4))
-            nc.sync.dma_start(out=x0[0][:], in_=x0T[0:P, :])
             with nc.allow_non_contiguous_dma(reason="one bias value a partition"):
                 nc.gpsimd.dma_start(out=b_raw[:], in_=b.rearrange("(c p) -> p c", p=P))
             nc.gpsimd.tensor_scalar(out=b1[:], in0=b_raw[:], scalar1=1.0, scalar2=None, op0=ALU.add)
 
             nc.vector.tensor_copy(out=g_sc[:], in_=tab_sc[:].bitcast(U8).indirect(offsets[:]))
+            nc.vector.tensor_copy(out=rows[0:32, 0 : J // 4], in_=g_sc[0:32, :].bitcast(I32))
             nc.vector.tensor_copy(
                 out=rows[:].bitcast(U8)[:, DN0 : DN0 + R].rearrange("p (t m) -> p t m", t=4),
                 in_=dn_sc_raw[:].bitcast(U8).rearrange("p (m t) -> p t m", t=4),
             )
-            nc.vector.tensor_copy(out=rows[0:32, 0 : J // 4], in_=g_sc[0:32, :].bitcast(I32))
-            for q in range(4):
-                nc.scalar.dma_start(out=planes[32 * q : 32 * q + 4, :, :], in_=rows[8 * q : 8 * q + 8, :])
-            nc.vector.tensor_copy(
-                out=dn_w[:].bitcast(U16).rearrange("p a (t m) -> p a t m", t=4),
-                in_=dn_raw[:].bitcast(U16).rearrange("p a (m t) -> p a t m", t=4),
-            )
+
+        for q in range(4):
+            nc.sync.dma_start(out=planes[32 * q : 32 * q + 4, :, :], in_=rows[8 * q : 8 * q + 8, :])
+        nc.vector.tensor_copy(
+            out=dn_w[:].bitcast(U16).rearrange("p a (t m) -> p a t m", t=4),
+            in_=dn_raw[:].bitcast(U16).rearrange("p a (m t) -> p a t m", t=4),
+        )
 
         late = ctx.enter_context(tc.tile_pool(name="late", bufs=1))
-        for c in range(1, NT):
+        x0 = []
+        for c in range(NT):
             x0c = late.tile([P, T], F32, name="x0_%d" % c)
             nc.sync.dma_start(out=x0c[:], in_=x0T[c * P : (c + 1) * P, :])
             x0.append(x0c)
@@ -133,6 +134,8 @@ def tile_list_xcross_relu_kernel(tc, tab_words, tab_scales, wb_words, wb_scales,
             nc.vector.quantize_mx(out=h_w[h][:].bitcast(FP8X4), scales=h_sc[h][:], in_=h_bf[h][:].rearrange("p j t -> p (j t)"))
 
         for c in range(NT):
+            yb = keep.tile([P, J], F32, name="yb_%d" % c)
+            res = keep.tile([P, J], F32, name="res_%d" % c)
             for h in range(HALVES):
                 y = ps_y.tile([P, HALF], F32, name="y")
                 for a in range(PASSES):
@@ -154,8 +157,13 @@ def tile_list_xcross_relu_kernel(tc, tab_words, tab_scales, wb_words, wb_scales,
                     start=False,
                     stop=True,
                 )
-                yb = keep.tile([P, HALF], F32, name="yb_%d_%d" % (c, h))
-                nc.scalar.activation(out=yb[:], in_=y[:], func=ACT.Identity, bias=b1[:, c : c + 1])
-                res = keep.tile([P, HALF], F32, name="res_%d_%d" % (c, h))
-                nc.vector.tensor_tensor(out=res[:], in0=x0[c][:].indirect(offs_of(h * HALF, HALF)), in1=yb[:], op=ALU.mult)
-                nc.sync.dma_start(out=out[c * P : (c + 1) * P, h * HALF : (h + 1) * HALF], in_=res[:])
+                nc.scalar.activation(out=yb[:, h * HALF : (h + 1) * HALF], in_=y[:], func=ACT.Identity, bias=b1[:, c : c + 1])
+            last = c == NT - 1
+            j0 = 0
+            for n in LAST_PIECES if last else [HALF, HALF]:
+                nc.vector.tensor_tensor(out=res[:, j0 : j0 + n], in0=x0[c][:].indirect(offs_of(j0, n)), in1=yb[:, j0 : j0 + n], op=ALU.mult)
+                if last:
+                    nc.sync.dma_start(out=out[c * P : (c + 1) * P, j0 : j0 + n], in_=res[:, j0 : j0 + n])
+                j0 += n
+            if not last:
+                nc.sync.dma_start(out=out[c * P : (c + 1) * P, :], in_=res[:])

@@ -1,6 +1,7 @@
 from contextlib import ExitStack
 
 import concourse.mybir as mybir
+from concourse.masks import make_identity
 
 K, R, N, T, J = 1024, 512, 512, 4096, 1024
 FLOPS = 2 * J * (K * R + K * N + R * N)
@@ -40,18 +41,22 @@ def tile_list_xcross_relu_kernel(tc, tab_words, tab_scales, wb_words, wb_scales,
 
         tab_sc = keep.tile([P, T // 4], I32, name="tab_sc", align_bytes=64)
         planes = keep.tile([P, PASSES, PLANE // 4], I32, name="planes", align_bytes=64)
-        nc.vector.memset(tab_sc[32:64, :], 0)
-        nc.vector.memset(tab_sc[64:128, :], 0)
-        nc.vector.memset(planes[:], 0)
         g_sc = keep.tile([P, J], U8, name="g_sc", align_bytes=64)
         dn_w = keep.tile([P, PASSES, 2 * R], U8, name="dn_w", align_bytes=64)
         tab_w = keep.tile([P, T], I32, name="tab_w", align_bytes=64)
         wb_w = keep.tile([P, PASSES, N // 2], I32, name="wb_w", align_bytes=64)
         rows = keep.tile([P, PLANE // 4], I32, name="rows", align_bytes=64)
         dn_raw = keep.tile([P, PASSES, R // 2], I32, name="dn_raw", align_bytes=64)
-        up_raw = keep.tile([P, 4, N], F32, name="up_raw")
-        b_raw = keep.tile([P, NT], F32, name="b_raw")
+        up_raw = keep.tile([P, 2, N], F32, name="up_raw")
+        up_rows = upw.rearrange("(p t) n -> p t n", t=4)
+        b_rows = keep.tile([P, P], F32, name="b_rows")
+        ident = keep.tile([P, P], F32, name="ident")
         b1 = keep.tile([P, NT], F32, name="b1")
+
+        nc.vector.memset(b_rows[:], 0.0)
+        nc.vector.memset(tab_sc[32:64, :], 0)
+        nc.vector.memset(tab_sc[64:128, :], 0)
+        nc.vector.memset(planes[:], 0)
 
         def scale_rows(scales):
             return scales.rearrange("a q n -> q a n").bitcast(I32)
@@ -66,10 +71,12 @@ def tile_list_xcross_relu_kernel(tc, tab_words, tab_scales, wb_words, wb_scales,
             nc.sync.dma_start(out=dn_raw[:], in_=dn_words.rearrange("a p w -> p a w").bitcast(I32))
             nc.sync.dma_start(out=tab_w[:], in_=tab_words[0].rearrange("p t c -> p (t c)").bitcast(I32))
             nc.sync.dma_start(out=wb_w[:], in_=wb_words.rearrange("a p w -> p a w").bitcast(I32))
-            nc.sync.dma_start(out=up_raw[:], in_=upw.rearrange("(p t) n -> p t n", t=4))
-            with nc.allow_non_contiguous_dma(reason="one bias value a partition"):
-                nc.gpsimd.dma_start(out=b_raw[:], in_=b.rearrange("(c p) -> p c", p=P))
-            nc.gpsimd.tensor_scalar(out=b1[:], in0=b_raw[:], scalar1=1.0, scalar2=None, op0=ALU.add)
+            nc.sync.dma_start(out=up_raw[:], in_=up_rows[:, 0:2, :])
+            nc.scalar.dma_start(out=b_rows[0:NT, :], in_=b.rearrange("(c p) -> c p", p=P))
+            make_identity(nc, ident[:])
+            b_cols = ps_y.tile([P, HALF], F32, name="y")
+            nc.tensor.transpose(b_cols[:, 0:P], b_rows[:], ident[:])
+            nc.scalar.activation(out=b1[:], in_=b_cols[:, 0:NT], func=ACT.Copy, bias=1.0)
 
             nc.vector.tensor_copy(out=g_sc[:], in_=tab_sc[:].bitcast(U8).indirect(offsets[:]))
             nc.vector.tensor_copy(out=rows[0:32, 0 : J // 4], in_=g_sc[0:32, :].bitcast(I32))
@@ -78,7 +85,7 @@ def tile_list_xcross_relu_kernel(tc, tab_words, tab_scales, wb_words, wb_scales,
                 in_=dn_sc_raw[:].bitcast(U8).rearrange("p (m t) -> p t m", t=4),
             )
 
-        for q in range(4):
+        for q in (0, 2, 1, 3):
             nc.sync.dma_start(out=planes[32 * q : 32 * q + 4, :, :], in_=rows[8 * q : 8 * q + 8, :])
         nc.vector.tensor_copy(
             out=dn_w[:].bitcast(U16).rearrange("p a (t m) -> p a t m", t=4),
@@ -86,6 +93,8 @@ def tile_list_xcross_relu_kernel(tc, tab_words, tab_scales, wb_words, wb_scales,
         )
 
         late = ctx.enter_context(tc.tile_pool(name="late", bufs=1))
+        up_raw2 = late.tile([P, 2, N], F32, name="up_raw2")
+        nc.sync.dma_start(out=up_raw2[:], in_=up_rows[:, 2:4, :])
         x0 = []
         for c in range(NT):
             x0c = late.tile([P, T], F32, name="x0_%d" % c)
@@ -98,19 +107,20 @@ def tile_list_xcross_relu_kernel(tc, tab_words, tab_scales, wb_words, wb_scales,
         def plane(a, c0, n):
             return planes[:, a, :].bitcast(U8)[:, c0 : c0 + n]
 
-        g_w = [keep.tile([P, HALF], U32, name="g_w_%d" % h, align_bytes=64) for h in range(HALVES)]
         t_w = [keep.tile([P, PASSES, 2 * HALF], U8, name="t_w_%d" % h, align_bytes=64) for h in range(HALVES)]
         for h in range(HALVES):
-            nc.vector.tensor_copy(out=g_w[h][:], in_=tab_w[:].bitcast(U32).indirect(offs_of(h * HALF, HALF)))
+            g_w = keep.tile([P, HALF], U32, name="g_w", align_bytes=64)
+            nc.vector.tensor_copy(out=g_w[:], in_=tab_w[:].bitcast(U32).indirect(offs_of(h * HALF, HALF)))
             nc.vector.tensor_copy(
                 out=t_w[h][:].bitcast(U16),
-                in_=g_w[h][:].bitcast(U16).rearrange("p (j d) -> p d j", d=PASSES),
+                in_=g_w[:].bitcast(U16).rearrange("p (j d) -> p d j", d=PASSES),
             )
 
         up_bf = keep.tile([P, N, 4], BF16, name="up_bf", align_bytes=64)
         up_w = keep.tile([P, N], U32, name="up_w", align_bytes=64)
         up_sc = keep.tile([P, N], U8, name="up_sc", align_bytes=64)
-        nc.vector.tensor_copy(out=up_bf[:], in_=up_raw[:].rearrange("p t n -> p n t"))
+        nc.vector.tensor_copy(out=up_bf[:, :, 0:2], in_=up_raw[:].rearrange("p t n -> p n t"))
+        nc.vector.tensor_copy(out=up_bf[:, :, 2:4], in_=up_raw2[:].rearrange("p t n -> p n t"))
         nc.vector.quantize_mx(out=up_w[:].bitcast(FP8X4), scales=up_sc[:], in_=up_bf[:].rearrange("p n t -> p (n t)"))
 
         h_bf = [keep.tile([P, HALF, 4], BF16, name="h_bf_%d" % h, align_bytes=64) for h in range(HALVES)]

@@ -26,6 +26,7 @@ NT = N // P
 DN0 = J
 WB0 = J + R
 PLANE = J + R + N
+S0 = 96
 LAST_PIECES = [512, 256, 256]
 
 
@@ -41,21 +42,18 @@ def tile_list_xcross_relu_kernel(tc, tab_words, tab_scales, wb_words, wb_scales,
 
         tab_sc = keep.tile([P, T // 4], I32, name="tab_sc", align_bytes=64)
         planes = keep.tile([P, PASSES, PLANE // 4], I32, name="planes", align_bytes=64)
-        g_sc = keep.tile([P, J], U8, name="g_sc", align_bytes=64)
         dn_w = keep.tile([P, PASSES, 2 * R], U8, name="dn_w", align_bytes=64)
         tab_w = keep.tile([P, T], I32, name="tab_w", align_bytes=64)
         wb_w = keep.tile([P, PASSES, N // 2], I32, name="wb_w", align_bytes=64)
-        rows = keep.tile([P, PLANE // 4], I32, name="rows", align_bytes=64)
         dn_raw = keep.tile([P, PASSES, R // 2], I32, name="dn_raw", align_bytes=64)
-        up_raw = keep.tile([P, 2, N], F32, name="up_raw")
-        up_rows = upw.rearrange("(p t) n -> p t n", t=4)
+        up_raw = keep.tile([P, 4, N], F32, name="up_raw")
         b_rows = keep.tile([P, P], F32, name="b_rows")
         ident = keep.tile([P, P], F32, name="ident")
         b1 = keep.tile([P, NT], F32, name="b1")
+        rows = keep.tile([P, PLANE // 4], I32, name="rows", align_bytes=64)
 
         nc.vector.memset(b_rows[:], 0.0)
-        nc.vector.memset(tab_sc[32:64, :], 0)
-        nc.vector.memset(tab_sc[64:128, :], 0)
+        nc.vector.memset(tab_sc[0:S0, :], 0)
         nc.vector.memset(planes[:], 0)
 
         def scale_rows(scales):
@@ -63,38 +61,36 @@ def tile_list_xcross_relu_kernel(tc, tab_words, tab_scales, wb_words, wb_scales,
 
         with tc.tile_pool(name="stage", bufs=1) as stage:
             dn_sc_raw = stage.tile([P, R // 4], I32, name="dn_sc_raw", align_bytes=64)
-            nc.vector.memset(dn_sc_raw[32:64, :], 0)
-            nc.vector.memset(dn_sc_raw[64:128, :], 0)
-            nc.sync.dma_start(out=tab_sc[0:32, :], in_=scale_rows(tab_scales))
-            nc.sync.dma_start(out=dn_sc_raw[0:32, :], in_=scale_rows(dn_scales))
-            nc.sync.dma_start(out=rows[0:32, WB0 // 4 : (WB0 + N) // 4], in_=scale_rows(wb_scales))
+            g_sc = stage.tile([P, J], U8, name="g_sc", align_bytes=64)
+            nc.vector.memset(dn_sc_raw[0:S0, :], 0)
+            nc.sync.dma_start(out=dn_sc_raw[S0:P, :], in_=scale_rows(dn_scales))
+            nc.sync.dma_start(out=tab_sc[S0:P, :], in_=scale_rows(tab_scales))
+            nc.sync.dma_start(out=rows[S0:P, WB0 // 4 : (WB0 + N) // 4], in_=scale_rows(wb_scales))
             nc.sync.dma_start(out=dn_raw[:], in_=dn_words.rearrange("a p w -> p a w").bitcast(I32))
+            nc.scalar.dma_start(out=b_rows[0:NT, :], in_=b.rearrange("(c p) -> c p", p=P))
             nc.sync.dma_start(out=tab_w[:], in_=tab_words[0].rearrange("p t c -> p (t c)").bitcast(I32))
             nc.sync.dma_start(out=wb_w[:], in_=wb_words.rearrange("a p w -> p a w").bitcast(I32))
-            nc.sync.dma_start(out=up_raw[:], in_=up_rows[:, 0:2, :])
-            nc.scalar.dma_start(out=b_rows[0:NT, :], in_=b.rearrange("(c p) -> c p", p=P))
+            nc.sync.dma_start(out=up_raw[:], in_=upw.rearrange("(p t) n -> p t n", t=4))
             make_identity(nc, ident[:])
             b_cols = ps_y.tile([P, HALF], F32, name="y")
             nc.tensor.transpose(b_cols[:, 0:P], b_rows[:], ident[:])
             nc.scalar.activation(out=b1[:], in_=b_cols[:, 0:NT], func=ACT.Copy, bias=1.0)
 
-            nc.vector.tensor_copy(out=g_sc[:], in_=tab_sc[:].bitcast(U8).indirect(offsets[:]))
-            nc.vector.tensor_copy(out=rows[0:32, 0 : J // 4], in_=g_sc[0:32, :].bitcast(I32))
             nc.vector.tensor_copy(
                 out=rows[:].bitcast(U8)[:, DN0 : DN0 + R].rearrange("p (t m) -> p t m", t=4),
                 in_=dn_sc_raw[:].bitcast(U8).rearrange("p (m t) -> p t m", t=4),
             )
+            nc.vector.tensor_copy(out=g_sc[:], in_=tab_sc[:].bitcast(U8).indirect(offsets[:]))
+            nc.vector.tensor_copy(out=rows[S0:P, 0 : J // 4], in_=g_sc[S0:P, :].bitcast(I32))
 
         for q in (0, 2, 1, 3):
-            nc.sync.dma_start(out=planes[32 * q : 32 * q + 4, :, :], in_=rows[8 * q : 8 * q + 8, :])
+            nc.sync.dma_start(out=planes[32 * q : 32 * q + 4, :, :], in_=rows[S0 + 8 * q : S0 + 8 * q + 8, :])
         nc.vector.tensor_copy(
             out=dn_w[:].bitcast(U16).rearrange("p a (t m) -> p a t m", t=4),
             in_=dn_raw[:].bitcast(U16).rearrange("p a (m t) -> p a t m", t=4),
         )
 
         late = ctx.enter_context(tc.tile_pool(name="late", bufs=1))
-        up_raw2 = late.tile([P, 2, N], F32, name="up_raw2")
-        nc.sync.dma_start(out=up_raw2[:], in_=up_rows[:, 2:4, :])
         x0 = []
         for c in range(NT):
             x0c = late.tile([P, T], F32, name="x0_%d" % c)
@@ -119,8 +115,10 @@ def tile_list_xcross_relu_kernel(tc, tab_words, tab_scales, wb_words, wb_scales,
         up_bf = keep.tile([P, N, 4], BF16, name="up_bf", align_bytes=64)
         up_w = keep.tile([P, N], U32, name="up_w", align_bytes=64)
         up_sc = keep.tile([P, N], U8, name="up_sc", align_bytes=64)
-        nc.vector.tensor_copy(out=up_bf[:, :, 0:2], in_=up_raw[:].rearrange("p t n -> p n t"))
-        nc.vector.tensor_copy(out=up_bf[:, :, 2:4], in_=up_raw2[:].rearrange("p t n -> p n t"))
+        nc.vector.tensor_copy(
+            out=up_bf[:].rearrange("p (c i) t -> p c t i", i=4),
+            in_=up_raw[:].rearrange("p t (c i) -> p c t i", i=4),
+        )
         nc.vector.quantize_mx(out=up_w[:].bitcast(FP8X4), scales=up_sc[:], in_=up_bf[:].rearrange("p n t -> p (n t)"))
 
         h_bf = [keep.tile([P, HALF, 4], BF16, name="h_bf_%d" % h, align_bytes=64) for h in range(HALVES)]

@@ -26,8 +26,7 @@ NT = N // P
 DN0 = J
 WB0 = J + R
 PLANE = J + R + N
-S0 = 96
-LAST_PIECES = [512, 256, 256]
+LAST_PIECES = [512, 256, 128, 128]
 
 
 def tile_list_xcross_relu_kernel(tc, tab_words, tab_scales, wb_words, wb_scales, dn_words, dn_scales, upw, x0T, b, offs, out):
@@ -41,37 +40,43 @@ def tile_list_xcross_relu_kernel(tc, tab_words, tab_scales, wb_words, wb_scales,
         nc.sync.dma_start(offsets[:], offs)
 
         tab_sc = keep.tile([P, T // 4], I32, name="tab_sc", align_bytes=64)
-        planes = keep.tile([P, PASSES, PLANE // 4], I32, name="planes", align_bytes=64)
         dn_w = keep.tile([P, PASSES, 2 * R], U8, name="dn_w", align_bytes=64)
-        tab_w = keep.tile([P, T], I32, name="tab_w", align_bytes=64)
         wb_w = keep.tile([P, PASSES, N // 2], I32, name="wb_w", align_bytes=64)
         dn_raw = keep.tile([P, PASSES, R // 2], I32, name="dn_raw", align_bytes=64)
-        up_raw = keep.tile([P, 4, N], F32, name="up_raw")
         b_rows = keep.tile([P, P], F32, name="b_rows")
         ident = keep.tile([P, P], F32, name="ident")
         b1 = keep.tile([P, NT], F32, name="b1")
         rows = keep.tile([P, PLANE // 4], I32, name="rows", align_bytes=64)
 
-        nc.vector.memset(b_rows[:], 0.0)
-        nc.vector.memset(tab_sc[0:S0, :], 0)
-        nc.vector.memset(planes[:], 0)
+        dn_sc_raw = keep.tile([P, R // 4], I32, name="dn_sc_raw", align_bytes=64)
 
         def scale_rows(scales):
             return scales.rearrange("a q n -> q a n").bitcast(I32)
 
+        nc.vector.memset(tab_sc[:], 0)
+        nc.vector.memset(dn_sc_raw[:], 0)
+        nc.sync.dma_start(out=tab_sc[0:P:4, :], in_=scale_rows(tab_scales))
+        nc.sync.dma_start(out=dn_sc_raw[0:P:4, :], in_=scale_rows(dn_scales))
+        nc.sync.dma_start(out=rows[0:P:4, WB0 // 4 : (WB0 + N) // 4], in_=scale_rows(wb_scales))
+        nc.sync.dma_start(out=dn_raw[:], in_=dn_words.rearrange("a p w -> p a w").bitcast(I32))
+        nc.sync.dma_start(out=wb_w[:], in_=wb_words.rearrange("a p w -> p a w").bitcast(I32))
+
+        mid = ctx.enter_context(tc.tile_pool(name="mid", bufs=1))
+        zeros = mid.tile([P, PASSES * PLANE // 4 + P], F32, name="zeros", offset=4 * T - 256)
+        nc.vector.memset(zeros[:, 0:P], 0.0)
+        nc.vector.tensor_copy(out=b_rows[:], in_=zeros[:, 0:P])
+        make_identity(nc, ident[:])
+        planes = mid.tile([P, PASSES, PLANE // 4], I32, name="planes", align_bytes=64, offset=4 * T)
+        nc.vector.memset(planes[:], 0)
+        nc.scalar.dma_start(out=b_rows[0:NT, :], in_=b.rearrange("(c p) -> c p", p=P))
+
+        tab_w = mid.tile([P, T], I32, name="tab_w", align_bytes=64, offset=0)
+        up_raw = mid.tile([P, 4, N], F32, name="up_raw", offset=4 * T + PASSES * PLANE)
+        nc.sync.dma_start(out=tab_w[:], in_=tab_words[0].rearrange("p t c -> p (t c)").bitcast(I32))
+        nc.sync.dma_start(out=up_raw[:], in_=upw.rearrange("(p t) n -> p t n", t=4))
+
         with tc.tile_pool(name="stage", bufs=1) as stage:
-            dn_sc_raw = stage.tile([P, R // 4], I32, name="dn_sc_raw", align_bytes=64)
             g_sc = stage.tile([P, J], U8, name="g_sc", align_bytes=64)
-            nc.vector.memset(dn_sc_raw[0:S0, :], 0)
-            nc.sync.dma_start(out=dn_sc_raw[S0:P, :], in_=scale_rows(dn_scales))
-            nc.sync.dma_start(out=tab_sc[S0:P, :], in_=scale_rows(tab_scales))
-            nc.sync.dma_start(out=rows[S0:P, WB0 // 4 : (WB0 + N) // 4], in_=scale_rows(wb_scales))
-            nc.sync.dma_start(out=dn_raw[:], in_=dn_words.rearrange("a p w -> p a w").bitcast(I32))
-            nc.scalar.dma_start(out=b_rows[0:NT, :], in_=b.rearrange("(c p) -> c p", p=P))
-            nc.sync.dma_start(out=tab_w[:], in_=tab_words[0].rearrange("p t c -> p (t c)").bitcast(I32))
-            nc.sync.dma_start(out=wb_w[:], in_=wb_words.rearrange("a p w -> p a w").bitcast(I32))
-            nc.sync.dma_start(out=up_raw[:], in_=upw.rearrange("(p t) n -> p t n", t=4))
-            make_identity(nc, ident[:])
             b_cols = ps_y.tile([P, HALF], F32, name="y")
             nc.tensor.transpose(b_cols[:, 0:P], b_rows[:], ident[:])
             nc.scalar.activation(out=b1[:], in_=b_cols[:, 0:NT], func=ACT.Copy, bias=1.0)
@@ -81,10 +86,10 @@ def tile_list_xcross_relu_kernel(tc, tab_words, tab_scales, wb_words, wb_scales,
                 in_=dn_sc_raw[:].bitcast(U8).rearrange("p (m t) -> p t m", t=4),
             )
             nc.vector.tensor_copy(out=g_sc[:], in_=tab_sc[:].bitcast(U8).indirect(offsets[:]))
-            nc.vector.tensor_copy(out=rows[S0:P, 0 : J // 4], in_=g_sc[S0:P, :].bitcast(I32))
+            nc.vector.tensor_copy(out=rows[:, 0 : J // 4], in_=g_sc[:].bitcast(I32))
 
         for q in (0, 2, 1, 3):
-            nc.sync.dma_start(out=planes[32 * q : 32 * q + 4, :, :], in_=rows[S0 + 8 * q : S0 + 8 * q + 8, :])
+            nc.sync.dma_start(out=planes[32 * q : 32 * q + 4, :, :], in_=rows[32 * q : 32 * q + 32 : 4, :])
         nc.vector.tensor_copy(
             out=dn_w[:].bitcast(U16).rearrange("p a (t m) -> p a t m", t=4),
             in_=dn_raw[:].bitcast(U16).rearrange("p a (m t) -> p a t m", t=4),
@@ -105,7 +110,7 @@ def tile_list_xcross_relu_kernel(tc, tab_words, tab_scales, wb_words, wb_scales,
 
         t_w = [keep.tile([P, PASSES, 2 * HALF], U8, name="t_w_%d" % h, align_bytes=64) for h in range(HALVES)]
         for h in range(HALVES):
-            g_w = keep.tile([P, HALF], U32, name="g_w", align_bytes=64)
+            g_w = late.tile([P, HALF], U32, name="g_w", align_bytes=64)
             nc.vector.tensor_copy(out=g_w[:], in_=tab_w[:].bitcast(U32).indirect(offs_of(h * HALF, HALF)))
             nc.vector.tensor_copy(
                 out=t_w[h][:].bitcast(U16),

@@ -129,7 +129,10 @@ def tile_list_xcross_relu_kernel(tc, tab_words, tab_scales, wb_words, wb_scales,
         h_bf = [keep.tile([P, HALF, 4], BF16, name="h_bf_%d" % h, align_bytes=64) for h in range(HALVES)]
         h_w = [keep.tile([P, HALF], U32, name="h_w_%d" % h, align_bytes=64) for h in range(HALVES)]
         h_sc = [keep.tile([P, HALF], U8, name="h_sc_%d" % h, align_bytes=64) for h in range(HALVES)]
-        for h in range(HALVES):
+        yb = [keep.tile([P, J], F32, name="yb_%d" % c) for c in range(NT)]
+        res = [keep.tile([P, J], F32, name="res_%d" % c) for c in range(NT)]
+
+        def hidden(h):
             for j0 in range(0, HALF, CH):
                 hs = ps_h.tile([P, 4, CH], F32, name="hs")
                 for t in range(4):
@@ -146,37 +149,53 @@ def tile_list_xcross_relu_kernel(tc, tab_words, tab_scales, wb_words, wb_scales,
                 nc.scalar.activation(out=h_bf[h][:, j0 : j0 + CH, :], in_=hs[:].rearrange("p t n -> p n t"), func=ACT.Relu)
             nc.vector.quantize_mx(out=h_w[h][:].bitcast(FP8X4), scales=h_sc[h][:], in_=h_bf[h][:].rearrange("p j t -> p (j t)"))
 
-        for c in range(NT):
-            yb = keep.tile([P, J], F32, name="yb_%d" % c)
-            res = keep.tile([P, J], F32, name="res_%d" % c)
-            for h in range(HALVES):
-                y = ps_y.tile([P, HALF], F32, name="y")
-                for a in range(PASSES):
-                    nc.tensor.matmul_mx(
-                        out=y[:],
-                        lhsT=wb_w[:, a, :].bitcast(U8)[:, 2 * P * c : 2 * P * (c + 1)].bitcast(FP4X4),
-                        lhsT_scale=plane(a, WB0 + P * c, P),
-                        rhs=t_w[h][:, a, :].bitcast(FP4X4),
-                        rhs_scale=plane(a, h * HALF, HALF),
-                        start=(a == 0),
-                        stop=False,
-                    )
+        def sums(c, h):
+            y = ps_y.tile([P, HALF], F32, name="y")
+            for a in range(PASSES):
                 nc.tensor.matmul_mx(
                     out=y[:],
-                    lhsT=up_w[:, P * c : P * (c + 1)].bitcast(FP8X4),
-                    lhsT_scale=up_sc[:, P * c : P * (c + 1)],
-                    rhs=h_w[h][:].bitcast(FP8X4),
-                    rhs_scale=h_sc[h][:],
-                    start=False,
-                    stop=True,
+                    lhsT=wb_w[:, a, :].bitcast(U8)[:, 2 * P * c : 2 * P * (c + 1)].bitcast(FP4X4),
+                    lhsT_scale=plane(a, WB0 + P * c, P),
+                    rhs=t_w[h][:, a, :].bitcast(FP4X4),
+                    rhs_scale=plane(a, h * HALF, HALF),
+                    start=(a == 0),
+                    stop=False,
                 )
-                nc.scalar.activation(out=yb[:, h * HALF : (h + 1) * HALF], in_=y[:], func=ACT.Identity, bias=b1[:, c : c + 1])
-            last = c == NT - 1
-            j0 = 0
-            for n in LAST_PIECES if last else [HALF, HALF]:
-                nc.vector.tensor_tensor(out=res[:, j0 : j0 + n], in0=x0[c][:].indirect(offs_of(j0, n)), in1=yb[:, j0 : j0 + n], op=ALU.mult)
-                if last:
-                    nc.sync.dma_start(out=out[c * P : (c + 1) * P, j0 : j0 + n], in_=res[:, j0 : j0 + n])
-                j0 += n
-            if not last:
-                nc.sync.dma_start(out=out[c * P : (c + 1) * P, :], in_=res[:])
+            nc.tensor.matmul_mx(
+                out=y[:],
+                lhsT=up_w[:, P * c : P * (c + 1)].bitcast(FP8X4),
+                lhsT_scale=up_sc[:, P * c : P * (c + 1)],
+                rhs=h_w[h][:].bitcast(FP8X4),
+                rhs_scale=h_sc[h][:],
+                start=False,
+                stop=True,
+            )
+            nc.scalar.activation(out=yb[c][:, h * HALF : (h + 1) * HALF], in_=y[:], func=ACT.Identity, bias=b1[:, c : c + 1])
+
+        def cross(c, j0, n):
+            nc.vector.tensor_tensor(out=res[c][:, j0 : j0 + n], in0=x0[c][:].indirect(offs_of(j0, n)), in1=yb[c][:, j0 : j0 + n], op=ALU.mult)
+
+        def store(c, j0, n):
+            nc.sync.dma_start(out=out[c * P : (c + 1) * P, j0 : j0 + n], in_=res[c][:, j0 : j0 + n])
+
+        hidden(0)
+        sums(0, 0)
+        sums(1, 0)
+        hidden(1)
+        cross(0, 0, HALF)
+        cross(1, 0, HALF)
+        for c in range(2):
+            sums(c, 1)
+            cross(c, HALF, HALF)
+            store(c, 0, J)
+        for h in range(HALVES):
+            sums(2, h)
+            cross(2, h * HALF, HALF)
+        store(2, 0, J)
+        for h in range(HALVES):
+            sums(3, h)
+        j0 = 0
+        for n in LAST_PIECES:
+            cross(3, j0, n)
+            store(3, j0, n)
+            j0 += n

@@ -41,8 +41,8 @@ def tile_list_xcross_relu_kernel(tc, tab_words, tab_scales, wb_words, wb_scales,
 
         tab_sc = keep.tile([P, T // 4], I32, name="tab_sc", align_bytes=64)
         dn_w = keep.tile([P, PASSES, 2 * R], U8, name="dn_w", align_bytes=64)
-        wb_w = keep.tile([P, PASSES, N // 2], I32, name="wb_w", align_bytes=64)
-        dn_raw = keep.tile([P, PASSES, R // 2], I32, name="dn_raw", align_bytes=64)
+        up_raw = keep.tile([P, 4, N], F32, name="up_raw")
+        nc.sync.dma_start(out=up_raw[:], in_=upw.rearrange("(p t) n -> p t n", t=4))
         b_rows = keep.tile([P, P], F32, name="b_rows")
         ident = keep.tile([P, P], F32, name="ident")
         b1 = keep.tile([P, NT], F32, name="b1")
@@ -58,11 +58,9 @@ def tile_list_xcross_relu_kernel(tc, tab_words, tab_scales, wb_words, wb_scales,
         nc.sync.dma_start(out=tab_sc[0:P:4, :], in_=scale_rows(tab_scales))
         nc.sync.dma_start(out=dn_sc_raw[0:P:4, :], in_=scale_rows(dn_scales))
         nc.sync.dma_start(out=rows[0:P:4, WB0 // 4 : (WB0 + N) // 4], in_=scale_rows(wb_scales))
-        nc.sync.dma_start(out=dn_raw[:], in_=dn_words.rearrange("a p w -> p a w").bitcast(I32))
-        nc.sync.dma_start(out=wb_w[:], in_=wb_words.rearrange("a p w -> p a w").bitcast(I32))
 
         mid = ctx.enter_context(tc.tile_pool(name="mid", bufs=1))
-        zeros = mid.tile([P, PASSES * PLANE // 4 + P], F32, name="zeros", offset=4 * T - 256)
+        zeros = mid.tile([P, PASSES * (PLANE + 2 * R) // 4 + P], F32, name="zeros", offset=4 * T - 256)
         nc.vector.memset(zeros[:, 0:P], 0.0)
         nc.vector.tensor_copy(out=b_rows[:], in_=zeros[:, 0:P])
         make_identity(nc, ident[:])
@@ -71,9 +69,11 @@ def tile_list_xcross_relu_kernel(tc, tab_words, tab_scales, wb_words, wb_scales,
         nc.scalar.dma_start(out=b_rows[0:NT, :], in_=b.rearrange("(c p) -> c p", p=P))
 
         tab_w = mid.tile([P, T], I32, name="tab_w", align_bytes=64, offset=0)
-        up_raw = mid.tile([P, 4, N], F32, name="up_raw", offset=4 * T + PASSES * PLANE)
+        dn_raw = mid.tile([P, PASSES, R // 2], I32, name="dn_raw", align_bytes=64, offset=4 * T + PASSES * PLANE)
+        wb_w = mid.tile([P, PASSES, N // 2], I32, name="wb_w", align_bytes=64, offset=4 * T + PASSES * (PLANE + 2 * R))
+        nc.sync.dma_start(out=dn_raw[:], in_=dn_words.rearrange("a p w -> p a w").bitcast(I32))
         nc.sync.dma_start(out=tab_w[:], in_=tab_words[0].rearrange("p t c -> p (t c)").bitcast(I32))
-        nc.sync.dma_start(out=up_raw[:], in_=upw.rearrange("(p t) n -> p t n", t=4))
+        nc.sync.dma_start(out=wb_w[:], in_=wb_words.rearrange("a p w -> p a w").bitcast(I32))
 
         with tc.tile_pool(name="stage", bufs=1) as stage:
             g_sc = stage.tile([P, J], U8, name="g_sc", align_bytes=64)
@@ -118,11 +118,12 @@ def tile_list_xcross_relu_kernel(tc, tab_words, tab_scales, wb_words, wb_scales,
             )
 
         up_bf = keep.tile([P, N, 4], BF16, name="up_bf", align_bytes=64)
-        up_w = keep.tile([P, N], U32, name="up_w", align_bytes=64)
+        up_w = late.tile([P, N], U32, name="up_w", align_bytes=64)
         up_sc = keep.tile([P, N], U8, name="up_sc", align_bytes=64)
-        nc.vector.tensor_copy(
+        nc.scalar.activation(
             out=up_bf[:].rearrange("p (c i) t -> p c t i", i=4),
             in_=up_raw[:].rearrange("p t (c i) -> p c t i", i=4),
+            func=ACT.Copy,
         )
         nc.vector.quantize_mx(out=up_w[:].bitcast(FP8X4), scales=up_sc[:], in_=up_bf[:].rearrange("p n t -> p (n t)"))
 

@@ -26,7 +26,7 @@ NT = N // P
 DN0 = J
 WB0 = J + R
 PLANE = J + R + N
-LAST_PIECES = [512, 256, 128, 128]
+LAST_PIECES = [640, 256, 128]
 
 
 def tile_list_xcross_relu_kernel(tc, tab_words, tab_scales, wb_words, wb_scales, dn_words, dn_scales, upw, x0T, b, offs, out):
@@ -53,10 +53,10 @@ def tile_list_xcross_relu_kernel(tc, tab_words, tab_scales, wb_words, wb_scales,
         def scale_rows(scales):
             return scales.rearrange("a q n -> q a n").bitcast(I32)
 
-        nc.vector.memset(tab_sc[:], 0)
         nc.vector.memset(dn_sc_raw[:], 0)
-        nc.sync.dma_start(out=tab_sc[0:P:4, :], in_=scale_rows(tab_scales))
+        nc.vector.memset(tab_sc[:], 0)
         nc.sync.dma_start(out=dn_sc_raw[0:P:4, :], in_=scale_rows(dn_scales))
+        nc.sync.dma_start(out=tab_sc[0:P:4, :], in_=scale_rows(tab_scales))
         nc.sync.dma_start(out=rows[0:P:4, WB0 // 4 : (WB0 + N) // 4], in_=scale_rows(wb_scales))
 
         mid = ctx.enter_context(tc.tile_pool(name="mid", bufs=1))

@@ -37,12 +37,12 @@ def tile_list_xcross_relu_kernel(tc, tab_words, tab_scales, wb_words, wb_scales,
         ps_y = ctx.enter_context(tc.psum_pool(name="ps_y", bufs=5))
 
         offsets = keep.tile([P, J // 16], U16, name="offsets")
-        nc.sync.dma_start(offsets[:], offs)
 
         tab_sc = keep.tile([P, T // 4], I32, name="tab_sc", align_bytes=64)
         dn_w = keep.tile([P, PASSES, 2 * R], U8, name="dn_w", align_bytes=64)
         up_raw = keep.tile([P, 4, N], F32, name="up_raw")
         nc.sync.dma_start(out=up_raw[:], in_=upw.rearrange("(p t) n -> p t n", t=4))
+        nc.sync.dma_start(offsets[:], offs)
         b_rows = keep.tile([P, P], F32, name="b_rows")
         ident = keep.tile([P, P], F32, name="ident")
         b1 = keep.tile([P, NT], F32, name="b1")
@@ -53,20 +53,20 @@ def tile_list_xcross_relu_kernel(tc, tab_words, tab_scales, wb_words, wb_scales,
         def scale_rows(scales):
             return scales.rearrange("a q n -> q a n").bitcast(I32)
 
+        nc.sync.dma_start(out=rows[0:P:4, WB0 // 4 : (WB0 + N) // 4], in_=scale_rows(wb_scales))
+        nc.scalar.dma_start(out=b_rows[P - NT : P, :], in_=b.rearrange("(c p) -> c p", p=P))
         nc.vector.memset(dn_sc_raw[:], 0)
         nc.vector.memset(tab_sc[:], 0)
         nc.sync.dma_start(out=dn_sc_raw[0:P:4, :], in_=scale_rows(dn_scales))
         nc.sync.dma_start(out=tab_sc[0:P:4, :], in_=scale_rows(tab_scales))
-        nc.sync.dma_start(out=rows[0:P:4, WB0 // 4 : (WB0 + N) // 4], in_=scale_rows(wb_scales))
 
         mid = ctx.enter_context(tc.tile_pool(name="mid", bufs=1))
         zeros = mid.tile([P, PASSES * (PLANE + 2 * R) // 4 + P], F32, name="zeros", offset=4 * T - 256)
         nc.vector.memset(zeros[:, 0:P], 0.0)
-        nc.vector.tensor_copy(out=b_rows[:], in_=zeros[:, 0:P])
+        nc.vector.tensor_copy(out=b_rows[0 : P - NT, :], in_=zeros[0 : P - NT, 0:P])
         make_identity(nc, ident[:])
         planes = mid.tile([P, PASSES, PLANE // 4], I32, name="planes", align_bytes=64, offset=4 * T)
         nc.vector.memset(planes[:], 0)
-        nc.scalar.dma_start(out=b_rows[0:NT, :], in_=b.rearrange("(c p) -> c p", p=P))
 
         tab_w = mid.tile([P, T], I32, name="tab_w", align_bytes=64, offset=0)
         dn_raw = mid.tile([P, PASSES, R // 2], I32, name="dn_raw", align_bytes=64, offset=4 * T + PASSES * PLANE)
@@ -79,7 +79,7 @@ def tile_list_xcross_relu_kernel(tc, tab_words, tab_scales, wb_words, wb_scales,
             g_sc = stage.tile([P, J], U8, name="g_sc", align_bytes=64)
             b_cols = ps_y.tile([P, HALF], F32, name="y")
             nc.tensor.transpose(b_cols[:, 0:P], b_rows[:], ident[:])
-            nc.scalar.activation(out=b1[:], in_=b_cols[:, 0:NT], func=ACT.Copy, bias=1.0)
+            nc.scalar.activation(out=b1[:], in_=b_cols[:, P - NT : P], func=ACT.Copy, bias=1.0)
 
             nc.vector.tensor_copy(
                 out=rows[:].bitcast(U8)[:, DN0 : DN0 + R].rearrange("p (t m) -> p t m", t=4),

@@ -55,14 +55,14 @@ def tile_list_xcross_relu_kernel(tc, tab_words, tab_scales, wb_words, wb_scales,
 
         nc.sync.dma_start(out=rows[0:P:4, WB0 // 4 : (WB0 + N) // 4], in_=scale_rows(wb_scales))
         nc.scalar.dma_start(out=b_rows[P - NT : P, :], in_=b.rearrange("(c p) -> c p", p=P))
-        nc.vector.memset(dn_sc_raw[:], 0)
+        nc.gpsimd.memset(dn_sc_raw[:], 0)
         nc.vector.memset(tab_sc[:], 0)
         nc.sync.dma_start(out=dn_sc_raw[0:P:4, :], in_=scale_rows(dn_scales))
         nc.sync.dma_start(out=tab_sc[0:P:4, :], in_=scale_rows(tab_scales))
 
         mid = ctx.enter_context(tc.tile_pool(name="mid", bufs=1))
         zeros = mid.tile([P, PASSES * (PLANE + 2 * R) // 4 + P], F32, name="zeros", offset=4 * T - 256)
-        nc.vector.memset(zeros[:, 0:P], 0.0)
+        nc.gpsimd.memset(zeros[:, 0:P], 0.0)
         nc.vector.tensor_copy(out=b_rows[0 : P - NT, :], in_=zeros[0 : P - NT, 0:P])
         make_identity(nc, ident[:])
         planes = mid.tile([P, PASSES, PLANE // 4], I32, name="planes", align_bytes=64, offset=4 * T)

@@ -130,7 +130,7 @@ def tile_list_xcross_relu_kernel(tc, tab_words, tab_scales, wb_words, wb_scales,
         h_bf = [keep.tile([P, HALF, 4], BF16, name="h_bf_%d" % h, align_bytes=64) for h in range(HALVES)]
         h_w = [keep.tile([P, HALF], U32, name="h_w_%d" % h, align_bytes=64) for h in range(HALVES)]
         h_sc = [keep.tile([P, HALF], U8, name="h_sc_%d" % h, align_bytes=64) for h in range(HALVES)]
-        yb = [keep.tile([P, J], F32, name="yb_%d" % c) for c in range(NT)]
+        yb = [None] + [keep.tile([P, J], F32, name="yb_%d" % c) for c in range(1, NT)]
         res = [keep.tile([P, J], F32, name="res_%d" % c) for c in range(NT)]
 
         def hidden(h):
@@ -149,6 +149,10 @@ def tile_list_xcross_relu_kernel(tc, tab_words, tab_scales, wb_words, wb_scales,
                         )
                 nc.scalar.activation(out=h_bf[h][:, j0 : j0 + CH, :], in_=hs[:].rearrange("p t n -> p n t"), func=ACT.Relu)
             nc.vector.quantize_mx(out=h_w[h][:].bitcast(FP8X4), scales=h_sc[h][:], in_=h_bf[h][:].rearrange("p j t -> p (j t)"))
+
+        g0 = keep.tile([P, J], F32, name="g0")
+        for h in range(HALVES):
+            nc.vector.tensor_copy(out=g0[:, h * HALF : (h + 1) * HALF], in_=x0[0][:].indirect(offs_of(h * HALF, HALF)))
 
         def sums(c, h):
             y = ps_y.tile([P, HALF], F32, name="y")
@@ -171,7 +175,12 @@ def tile_list_xcross_relu_kernel(tc, tab_words, tab_scales, wb_words, wb_scales,
                 start=False,
                 stop=True,
             )
-            nc.scalar.activation(out=yb[c][:, h * HALF : (h + 1) * HALF], in_=y[:], func=ACT.Identity, bias=b1[:, c : c + 1])
+            if c == 0:
+                nc.vector.scalar_tensor_tensor(
+                    out=res[0][:, h * HALF : (h + 1) * HALF], in0=y[:], scalar=b1[:, 0:1], in1=g0[:, h * HALF : (h + 1) * HALF], op0=ALU.add, op1=ALU.mult
+                )
+            else:
+                nc.scalar.activation(out=yb[c][:, h * HALF : (h + 1) * HALF], in_=y[:], func=ACT.Identity, bias=b1[:, c : c + 1])
 
         def cross(c, j0, n):
             nc.vector.tensor_tensor(out=res[c][:, j0 : j0 + n], in0=x0[c][:].indirect(offs_of(j0, n)), in1=yb[c][:, j0 : j0 + n], op=ALU.mult)
@@ -183,12 +192,12 @@ def tile_list_xcross_relu_kernel(tc, tab_words, tab_scales, wb_words, wb_scales,
         sums(0, 0)
         sums(1, 0)
         hidden(1)
-        cross(0, 0, HALF)
         cross(1, 0, HALF)
-        for c in range(2):
-            sums(c, 1)
-            cross(c, HALF, HALF)
-            store(c, 0, J)
+        sums(0, 1)
+        store(0, 0, J)
+        sums(1, 1)
+        cross(1, HALF, HALF)
+        store(1, 0, J)
         for h in range(HALVES):
             sums(2, h)
             cross(2, h * HALF, HALF)

@@ -38,17 +38,17 @@ def tile_list_xcross_relu_kernel(tc, tab_words, tab_scales, wb_words, wb_scales,
 
         offsets = keep.tile([P, J // 16], U16, name="offsets")
 
-        tab_sc = keep.tile([P, T // 4], I32, name="tab_sc", align_bytes=64)
+        tab_sc = keep.tile([P, T // 4], I32, name="tab_sc", align_bytes=256)
         dn_w = keep.tile([P, PASSES, 2 * R], U8, name="dn_w", align_bytes=64)
-        up_raw = keep.tile([P, 4, N], F32, name="up_raw")
+        up_raw = keep.tile([P, 4, N], F32, name="up_raw", align_bytes=256)
         nc.sync.dma_start(out=up_raw[:], in_=upw.rearrange("(p t) n -> p t n", t=4))
         nc.sync.dma_start(offsets[:], offs)
-        b_rows = keep.tile([P, P], F32, name="b_rows")
+        b_rows = keep.tile([P, P], F32, name="b_rows", align_bytes=256)
         ident = keep.tile([P, P], F32, name="ident")
         b1 = keep.tile([P, NT], F32, name="b1")
-        rows = keep.tile([P, PLANE // 4], I32, name="rows", align_bytes=64)
+        rows = keep.tile([P, PLANE // 4], I32, name="rows", align_bytes=256)
 
-        dn_sc_raw = keep.tile([P, R // 4], I32, name="dn_sc_raw", align_bytes=64)
+        dn_sc_raw = keep.tile([P, R // 4], I32, name="dn_sc_raw", align_bytes=256)
 
         def scale_rows(scales):
             return scales.rearrange("a q n -> q a n").bitcast(I32)
@@ -65,12 +65,12 @@ def tile_list_xcross_relu_kernel(tc, tab_words, tab_scales, wb_words, wb_scales,
         nc.gpsimd.memset(zeros[:, 0:P], 0.0)
         nc.vector.tensor_copy(out=b_rows[0 : P - NT, :], in_=zeros[0 : P - NT, 0:P])
         make_identity(nc, ident[:])
-        planes = mid.tile([P, PASSES, PLANE // 4], I32, name="planes", align_bytes=64, offset=4 * T)
+        planes = mid.tile([P, PASSES, PLANE // 4], I32, name="planes", align_bytes=256, offset=4 * T)
         nc.vector.memset(planes[:], 0)
 
-        tab_w = mid.tile([P, T], I32, name="tab_w", align_bytes=64, offset=0)
-        dn_raw = mid.tile([P, PASSES, R // 2], I32, name="dn_raw", align_bytes=64, offset=4 * T + PASSES * PLANE)
-        wb_w = mid.tile([P, PASSES, N // 2], I32, name="wb_w", align_bytes=64, offset=4 * T + PASSES * (PLANE + 2 * R))
+        tab_w = mid.tile([P, T], I32, name="tab_w", align_bytes=256, offset=0)
+        dn_raw = mid.tile([P, PASSES, R // 2], I32, name="dn_raw", align_bytes=256, offset=4 * T + PASSES * PLANE)
+        wb_w = mid.tile([P, PASSES, N // 2], I32, name="wb_w", align_bytes=256, offset=4 * T + PASSES * (PLANE + 2 * R))
         nc.sync.dma_start(out=dn_raw[:], in_=dn_words.rearrange("a p w -> p a w").bitcast(I32))
         nc.sync.dma_start(out=tab_w[:], in_=tab_words[0].rearrange("p t c -> p (t c)").bitcast(I32))
         nc.sync.dma_start(out=wb_w[:], in_=wb_words.rearrange("a p w -> p a w").bitcast(I32))
@@ -98,7 +98,7 @@ def tile_list_xcross_relu_kernel(tc, tab_words, tab_scales, wb_words, wb_scales,
         late = ctx.enter_context(tc.tile_pool(name="late", bufs=1))
         x0 = []
         for c in range(NT):
-            x0c = late.tile([P, T], F32, name="x0_%d" % c)
+            x0c = late.tile([P, T], F32, name="x0_%d" % c, align_bytes=256)
             nc.sync.dma_start(out=x0c[:], in_=x0T[c * P : (c + 1) * P, :])
             x0.append(x0c)
 
@@ -131,7 +131,7 @@ def tile_list_xcross_relu_kernel(tc, tab_words, tab_scales, wb_words, wb_scales,
         h_w = [keep.tile([P, HALF], U32, name="h_w_%d" % h, align_bytes=64) for h in range(HALVES)]
         h_sc = [keep.tile([P, HALF], U8, name="h_sc_%d" % h, align_bytes=64) for h in range(HALVES)]
         yb = [None] + [keep.tile([P, J], F32, name="yb_%d" % c) for c in range(1, NT)]
-        res = [keep.tile([P, J], F32, name="res_%d" % c) for c in range(NT)]
+        res = [keep.tile([P, J], F32, name="res_%d" % c, align_bytes=256) for c in range(NT)]
 
         def hidden(h):
             for j0 in range(0, HALF, CH):

@@ -21,7 +21,7 @@ P = 128
 PASSES = 2
 HALF = 512
 HALVES = J // HALF
-CH = 128
+CH = 256
 NT = N // P
 DN0 = J
 WB0 = J + R
@@ -33,8 +33,8 @@ def tile_list_xcross_relu_kernel(tc, tab_words, tab_scales, wb_words, wb_scales,
     nc = tc.nc
     with ExitStack() as ctx:
         keep = ctx.enter_context(tc.tile_pool(name="keep", bufs=1))
-        ps_h = ctx.enter_context(tc.psum_pool(name="ps_h", bufs=3))
-        ps_y = ctx.enter_context(tc.psum_pool(name="ps_y", bufs=5))
+        ps_h = ctx.enter_context(tc.psum_pool(name="ps_h", bufs=4))
+        ps_y = ctx.enter_context(tc.psum_pool(name="ps_y", bufs=4))
 
         offsets = keep.tile([P, J // 16], U16, name="offsets")
 
@@ -135,19 +135,20 @@ def tile_list_xcross_relu_kernel(tc, tab_words, tab_scales, wb_words, wb_scales,
 
         def hidden(h):
             for j0 in range(0, HALF, CH):
-                hs = ps_h.tile([P, 4, CH], F32, name="hs")
-                for t in range(4):
-                    for a in range(PASSES):
-                        nc.tensor.matmul_mx(
-                            out=hs[:, t, :],
-                            lhsT=dn_w[:, a, 2 * P * t : 2 * P * (t + 1)].bitcast(FP4X4),
-                            lhsT_scale=plane(a, DN0 + P * t, P),
-                            rhs=t_w[h][:, a, 2 * j0 : 2 * (j0 + CH)].bitcast(FP4X4),
-                            rhs_scale=plane(a, h * HALF + j0, CH),
-                            start=(a == 0),
-                            stop=(a == PASSES - 1),
-                        )
-                nc.scalar.activation(out=h_bf[h][:, j0 : j0 + CH, :], in_=hs[:].rearrange("p t n -> p n t"), func=ACT.Relu)
+                for t0 in (0, 2):
+                    hs = ps_h.tile([P, 2, CH], F32, name="hs")
+                    for t in (t0, t0 + 1):
+                        for a in range(PASSES):
+                            nc.tensor.matmul_mx(
+                                out=hs[:, t - t0, :],
+                                lhsT=dn_w[:, a, 2 * P * t : 2 * P * (t + 1)].bitcast(FP4X4),
+                                lhsT_scale=plane(a, DN0 + P * t, P),
+                                rhs=t_w[h][:, a, 2 * j0 : 2 * (j0 + CH)].bitcast(FP4X4),
+                                rhs_scale=plane(a, h * HALF + j0, CH),
+                                start=(a == 0),
+                                stop=(a == PASSES - 1),
+                            )
+                    nc.scalar.activation(out=h_bf[h][:, j0 : j0 + CH, t0 : t0 + 2], in_=hs[:].rearrange("p t n -> p n t"), func=ACT.Relu)
             nc.vector.quantize_mx(out=h_w[h][:].bitcast(FP8X4), scales=h_sc[h][:], in_=h_bf[h][:].rearrange("p j t -> p (j t)"))
 
         g0 = keep.tile([P, J], F32, name="g0")
@@ -189,9 +190,9 @@ def tile_list_xcross_relu_kernel(tc, tab_words, tab_scales, wb_words, wb_scales,
             nc.sync.dma_start(out=out[c * P : (c + 1) * P, j0 : j0 + n], in_=res[c][:, j0 : j0 + n])
 
         hidden(0)
+        hidden(1)
         sums(0, 0)
         sums(1, 0)
-        hidden(1)
         cross(1, 0, HALF)
         sums(0, 1)
         store(0, 0, J)

@@ -26,6 +26,7 @@ NT = N // P
 DN0 = J
 WB0 = J + R
 PLANE = J + R + N
+UP_PART = 256
 LAST_PIECES = [640, 256, 128]
 
 
@@ -33,74 +34,73 @@ def tile_list_xcross_relu_kernel(tc, tab_words, tab_scales, wb_words, wb_scales,
     nc = tc.nc
     with ExitStack() as ctx:
         keep = ctx.enter_context(tc.tile_pool(name="keep", bufs=1))
-        ps_h = ctx.enter_context(tc.psum_pool(name="ps_h", bufs=4))
-        ps_y = ctx.enter_context(tc.psum_pool(name="ps_y", bufs=4))
+        psum = ctx.enter_context(tc.psum_pool(name="psum", bufs=8))
 
         offsets = keep.tile([P, J // 16], U16, name="offsets")
-
+        dn_raw = keep.tile([P, PASSES, R // 2], I32, name="dn_raw", align_bytes=256)
         tab_sc = keep.tile([P, T // 4], I32, name="tab_sc", align_bytes=256)
-        dn_w = keep.tile([P, PASSES, 2 * R], U8, name="dn_w", align_bytes=64)
-        up_raw = keep.tile([P, 4, N], F32, name="up_raw", align_bytes=256)
-        nc.sync.dma_start(out=up_raw[:], in_=upw.rearrange("(p t) n -> p t n", t=4))
-        nc.sync.dma_start(offsets[:], offs)
+        dn_sc_raw = keep.tile([P, R // 4], I32, name="dn_sc_raw", align_bytes=256)
+        staged = keep.tile([P, PLANE // 4], I32, name="staged", align_bytes=256)
+        planes = keep.tile([P, PASSES, PLANE // 4], I32, name="planes", align_bytes=256)
         b_rows = keep.tile([P, P], F32, name="b_rows", align_bytes=256)
         ident = keep.tile([P, P], F32, name="ident")
         b1 = keep.tile([P, NT], F32, name="b1")
-        rows = keep.tile([P, PLANE // 4], I32, name="rows", align_bytes=256)
-
-        dn_sc_raw = keep.tile([P, R // 4], I32, name="dn_sc_raw", align_bytes=256)
+        dn_w = keep.tile([P, PASSES, 2 * R], U8, name="dn_w", align_bytes=64)
 
         def scale_rows(scales):
             return scales.rearrange("a q n -> q a n").bitcast(I32)
 
-        nc.sync.dma_start(out=rows[0:P:4, WB0 // 4 : (WB0 + N) // 4], in_=scale_rows(wb_scales))
-        nc.scalar.dma_start(out=b_rows[P - NT : P, :], in_=b.rearrange("(c p) -> c p", p=P))
-        nc.gpsimd.memset(dn_sc_raw[:], 0)
-        nc.vector.memset(tab_sc[:], 0)
-        nc.sync.dma_start(out=dn_sc_raw[0:P:4, :], in_=scale_rows(dn_scales))
-        nc.sync.dma_start(out=tab_sc[0:P:4, :], in_=scale_rows(tab_scales))
-
         mid = ctx.enter_context(tc.tile_pool(name="mid", bufs=1))
-        zeros = mid.tile([P, PASSES * (PLANE + 2 * R) // 4 + P], F32, name="zeros", offset=4 * T - 256)
+        zeros = mid.tile([P, 2 * P], F32, name="zeros", offset=4 * T - 4 * P)
         nc.gpsimd.memset(zeros[:, 0:P], 0.0)
+        nc.vector.memset(tab_sc[:, 0 : T // 8], 0)
+        nc.gpsimd.memset(tab_sc[:, T // 8 : T // 4], 0)
+        nc.gpsimd.memset(dn_sc_raw[:], 0)
+        nc.sync.dma_start(out=dn_raw[:], in_=dn_words.rearrange("a p w -> p a w").bitcast(I32))
+        nc.sync.dma_start(offsets[:], offs)
+        nc.scalar.dma_start(out=b_rows[P - NT : P, :], in_=b.rearrange("(c p) -> c p", p=P))
+        nc.sync.dma_start(out=staged[0:P:4, WB0 // 4 : (WB0 + N) // 4], in_=scale_rows(wb_scales))
+        nc.sync.dma_start(out=tab_sc[0:P:4, :], in_=scale_rows(tab_scales))
+        nc.sync.dma_start(out=dn_sc_raw[0:P:4, :], in_=scale_rows(dn_scales))
+
         nc.vector.tensor_copy(out=b_rows[0 : P - NT, :], in_=zeros[0 : P - NT, 0:P])
         make_identity(nc, ident[:])
-        planes = mid.tile([P, PASSES, PLANE // 4], I32, name="planes", align_bytes=256, offset=4 * T)
         nc.vector.memset(planes[:], 0)
 
+        wb_w = mid.tile([P, PASSES, N // 2], I32, name="wb_w", align_bytes=256, offset=4 * T)
         tab_w = mid.tile([P, T], I32, name="tab_w", align_bytes=256, offset=0)
-        dn_raw = mid.tile([P, PASSES, R // 2], I32, name="dn_raw", align_bytes=256, offset=4 * T + PASSES * PLANE)
-        wb_w = mid.tile([P, PASSES, N // 2], I32, name="wb_w", align_bytes=256, offset=4 * T + PASSES * (PLANE + 2 * R))
-        nc.sync.dma_start(out=dn_raw[:], in_=dn_words.rearrange("a p w -> p a w").bitcast(I32))
         nc.sync.dma_start(out=tab_w[:], in_=tab_words[0].rearrange("p t c -> p (t c)").bitcast(I32))
         nc.sync.dma_start(out=wb_w[:], in_=wb_words.rearrange("a p w -> p a w").bitcast(I32))
 
-        with tc.tile_pool(name="stage", bufs=1) as stage:
-            g_sc = stage.tile([P, J], U8, name="g_sc", align_bytes=64)
-            b_cols = ps_y.tile([P, HALF], F32, name="y")
-            nc.tensor.transpose(b_cols[:, 0:P], b_rows[:], ident[:])
-            nc.scalar.activation(out=b1[:], in_=b_cols[:, P - NT : P], func=ACT.Copy, bias=1.0)
-
-            nc.vector.tensor_copy(
-                out=rows[:].bitcast(U8)[:, DN0 : DN0 + R].rearrange("p (t m) -> p t m", t=4),
-                in_=dn_sc_raw[:].bitcast(U8).rearrange("p (m t) -> p t m", t=4),
-            )
-            nc.vector.tensor_copy(out=g_sc[:], in_=tab_sc[:].bitcast(U8).indirect(offsets[:]))
-            nc.vector.tensor_copy(out=rows[:, 0 : J // 4], in_=g_sc[:].bitcast(I32))
-
-        for q in (0, 2, 1, 3):
-            nc.sync.dma_start(out=planes[32 * q : 32 * q + 4, :, :], in_=rows[32 * q : 32 * q + 32 : 4, :])
         nc.vector.tensor_copy(
             out=dn_w[:].bitcast(U16).rearrange("p a (t m) -> p a t m", t=4),
             in_=dn_raw[:].bitcast(U16).rearrange("p a (m t) -> p a t m", t=4),
         )
+        with tc.tile_pool(name="stage", bufs=1) as stage:
+            g_sc = stage.tile([P, J], U8, name="g_sc", align_bytes=64)
+            b_cols = psum.tile([P, HALF], F32, name="bank")
+            nc.tensor.transpose(b_cols[:, 0:P], b_rows[:], ident[:])
+            nc.scalar.activation(out=b1[:], in_=b_cols[:, P - NT : P], func=ACT.Copy, bias=1.0)
+
+            nc.vector.tensor_copy(out=g_sc[:], in_=tab_sc[:].bitcast(U8).indirect(offsets[:]))
+            nc.vector.tensor_copy(
+                out=staged[:].bitcast(U8)[:, DN0 : DN0 + R].rearrange("p (t m) -> p t m", t=4),
+                in_=dn_sc_raw[:].bitcast(U8).rearrange("p (m t) -> p t m", t=4),
+            )
+            nc.vector.tensor_copy(out=staged[:, 0 : J // 4], in_=g_sc[:].bitcast(I32))
+
+        for q in (0, 2, 1, 3):
+            nc.sync.dma_start(out=planes[32 * q : 32 * q + 4, :, :], in_=staged[32 * q : 32 * q + 32 : 4, :])
 
         late = ctx.enter_context(tc.tile_pool(name="late", bufs=1))
-        x0 = []
-        for c in range(NT):
-            x0c = late.tile([P, T], F32, name="x0_%d" % c, align_bytes=256)
-            nc.sync.dma_start(out=x0c[:], in_=x0T[c * P : (c + 1) * P, :])
-            x0.append(x0c)
+        x0_pair = late.tile([P, 2, T], F32, name="x0_pair", align_bytes=256)
+        nc.sync.dma_start(out=x0_pair[:], in_=x0T[0 : 2 * P, :].rearrange("(c p) t -> p c t", p=P))
+        up_raw = late.tile([P, 4, N], F32, name="up_raw", align_bytes=256)
+        nc.sync.dma_start(out=up_raw[:], in_=upw.rearrange("(p t) n -> p t n", t=4))
+        x0 = {}
+        for c in range(2, NT):
+            x0[c] = late.tile([P, T], F32, name="x0_%d" % c, align_bytes=256)
+            nc.sync.dma_start(out=x0[c][:], in_=x0T[c * P : (c + 1) * P, :])
 
         def offs_of(j0, n):
             return offsets[:, j0 // 16 : (j0 + n) // 16]
@@ -117,26 +117,13 @@ def tile_list_xcross_relu_kernel(tc, tab_words, tab_scales, wb_words, wb_scales,
                 in_=g_w[:].bitcast(U16).rearrange("p (j d) -> p d j", d=PASSES),
             )
 
-        up_bf = keep.tile([P, N, 4], BF16, name="up_bf", align_bytes=64)
-        up_w = late.tile([P, N], U32, name="up_w", align_bytes=64)
-        up_sc = keep.tile([P, N], U8, name="up_sc", align_bytes=64)
-        nc.scalar.activation(
-            out=up_bf[:].rearrange("p (c i) t -> p c t i", i=4),
-            in_=up_raw[:].rearrange("p t (c i) -> p c t i", i=4),
-            func=ACT.Copy,
-        )
-        nc.vector.quantize_mx(out=up_w[:].bitcast(FP8X4), scales=up_sc[:], in_=up_bf[:].rearrange("p n t -> p (n t)"))
-
         h_bf = [keep.tile([P, HALF, 4], BF16, name="h_bf_%d" % h, align_bytes=64) for h in range(HALVES)]
         h_w = [keep.tile([P, HALF], U32, name="h_w_%d" % h, align_bytes=64) for h in range(HALVES)]
         h_sc = [keep.tile([P, HALF], U8, name="h_sc_%d" % h, align_bytes=64) for h in range(HALVES)]
-        yb = [None] + [keep.tile([P, J], F32, name="yb_%d" % c) for c in range(1, NT)]
-        res = [keep.tile([P, J], F32, name="res_%d" % c, align_bytes=256) for c in range(NT)]
-
-        def hidden(h):
+        for h in range(HALVES):
             for j0 in range(0, HALF, CH):
                 for t0 in (0, 2):
-                    hs = ps_h.tile([P, 2, CH], F32, name="hs")
+                    hs = psum.tile([P, 2, CH], F32, name="bank")
                     for t in (t0, t0 + 1):
                         for a in range(PASSES):
                             nc.tensor.matmul_mx(
@@ -148,65 +135,80 @@ def tile_list_xcross_relu_kernel(tc, tab_words, tab_scales, wb_words, wb_scales,
                                 start=(a == 0),
                                 stop=(a == PASSES - 1),
                             )
-                    nc.scalar.activation(out=h_bf[h][:, j0 : j0 + CH, t0 : t0 + 2], in_=hs[:].rearrange("p t n -> p n t"), func=ACT.Relu)
+                    pairs = h_bf[h][:, j0 : j0 + CH, t0 : t0 + 2]
+                    if t0 == 0:
+                        nc.scalar.activation(out=pairs, in_=hs[:].rearrange("p t n -> p n t"), func=ACT.Relu)
+                    else:
+                        nc.vector.tensor_scalar_max(out=pairs, in0=hs[:].rearrange("p t n -> p n t"), scalar1=0.0)
             nc.vector.quantize_mx(out=h_w[h][:].bitcast(FP8X4), scales=h_sc[h][:], in_=h_bf[h][:].rearrange("p j t -> p (j t)"))
 
-        g0 = keep.tile([P, J], F32, name="g0")
-        for h in range(HALVES):
-            nc.vector.tensor_copy(out=g0[:, h * HALF : (h + 1) * HALF], in_=x0[0][:].indirect(offs_of(h * HALF, HALF)))
+        y = {}
+        for c in range(NT):
+            for h in range(HALVES):
+                y[c, h] = psum.tile([P, HALF], F32, name="bank")
+                for a in range(PASSES):
+                    nc.tensor.matmul_mx(
+                        out=y[c, h][:],
+                        lhsT=wb_w[:, a, :].bitcast(U8)[:, 2 * P * c : 2 * P * (c + 1)].bitcast(FP4X4),
+                        lhsT_scale=plane(a, WB0 + P * c, P),
+                        rhs=t_w[h][:, a, :].bitcast(FP4X4),
+                        rhs_scale=plane(a, h * HALF, HALF),
+                        start=(a == 0),
+                        stop=False,
+                    )
 
-        def sums(c, h):
-            y = ps_y.tile([P, HALF], F32, name="y")
-            for a in range(PASSES):
-                nc.tensor.matmul_mx(
-                    out=y[:],
-                    lhsT=wb_w[:, a, :].bitcast(U8)[:, 2 * P * c : 2 * P * (c + 1)].bitcast(FP4X4),
-                    lhsT_scale=plane(a, WB0 + P * c, P),
-                    rhs=t_w[h][:, a, :].bitcast(FP4X4),
-                    rhs_scale=plane(a, h * HALF, HALF),
-                    start=(a == 0),
-                    stop=False,
-                )
-            nc.tensor.matmul_mx(
-                out=y[:],
-                lhsT=up_w[:, P * c : P * (c + 1)].bitcast(FP8X4),
-                lhsT_scale=up_sc[:, P * c : P * (c + 1)],
-                rhs=h_w[h][:].bitcast(FP8X4),
-                rhs_scale=h_sc[h][:],
-                start=False,
-                stop=True,
+        g_0 = keep.tile([P, J], F32, name="h_bf_1", align_bytes=64)
+        nc.vector.tensor_copy(out=g_0[:], in_=x0_pair[:, 0, :].indirect(offsets[:]))
+        g_10 = keep.tile([P, HALF], F32, name="h_bf_0", align_bytes=64)
+        nc.vector.tensor_copy(out=g_10[:], in_=x0_pair[:, 1, :].indirect(offs_of(0, HALF)))
+        g = {(0, 0): g_0[:, 0:HALF], (0, 1): g_0[:, HALF:J], (1, 0): g_10[:]}
+
+        up_w, up_sc = [], []
+        for u in range(N // UP_PART):
+            up_bf = keep.tile([P, UP_PART, 4], BF16, name="up_bf_%d" % u, align_bytes=64)
+            up_w.append(keep.tile([P, UP_PART], U32, name="up_w_%d" % u, align_bytes=64))
+            up_sc.append(keep.tile([P, UP_PART], U8, name="up_sc_%d" % u, align_bytes=64))
+            nc.scalar.activation(
+                out=up_bf[:].rearrange("p (c i) t -> p c t i", i=4),
+                in_=up_raw[:, :, u * UP_PART : (u + 1) * UP_PART].rearrange("p t (c i) -> p c t i", i=4),
+                func=ACT.Copy,
             )
-            if c == 0:
-                nc.vector.scalar_tensor_tensor(
-                    out=res[0][:, h * HALF : (h + 1) * HALF], in0=y[:], scalar=b1[:, 0:1], in1=g0[:, h * HALF : (h + 1) * HALF], op0=ALU.add, op1=ALU.mult
+            nc.vector.quantize_mx(out=up_w[u][:].bitcast(FP8X4), scales=up_sc[u][:], in_=up_bf[:].rearrange("p n t -> p (n t)"))
+            if u == 0:
+                g_11 = keep.tile([P, HALF], F32, name="up_bf_0", align_bytes=64)
+                nc.vector.tensor_copy(out=g_11[:], in_=x0_pair[:, 1, :].indirect(offs_of(HALF, HALF)))
+                g[1, 1] = g_11[:]
+
+        res_pair = keep.tile([P, 2, J], F32, name="res_pair", align_bytes=256)
+        yb = {c: keep.tile([P, J], F32, name="yb_%d" % c) for c in range(2, NT)}
+        res = {c: keep.tile([P, J], F32, name="res_%d" % c, align_bytes=256) for c in range(2, NT)}
+        for c in range(NT):
+            u, n0 = divmod(c * P, UP_PART)
+            for h in range(HALVES):
+                cols = slice(h * HALF, (h + 1) * HALF)
+                nc.tensor.matmul_mx(
+                    out=y[c, h][:],
+                    lhsT=up_w[u][:, n0 : n0 + P].bitcast(FP8X4),
+                    lhsT_scale=up_sc[u][:, n0 : n0 + P],
+                    rhs=h_w[h][:].bitcast(FP8X4),
+                    rhs_scale=h_sc[h][:],
+                    start=False,
+                    stop=True,
                 )
-            else:
-                nc.scalar.activation(out=yb[c][:, h * HALF : (h + 1) * HALF], in_=y[:], func=ACT.Identity, bias=b1[:, c : c + 1])
+                if c < 2:
+                    nc.vector.scalar_tensor_tensor(
+                        out=res_pair[:, c, cols], in0=y[c, h][:], scalar=b1[:, c : c + 1], in1=g[c, h], op0=ALU.add, op1=ALU.mult
+                    )
+                else:
+                    nc.scalar.activation(out=yb[c][:, cols], in_=y[c, h][:], func=ACT.Identity, bias=b1[:, c : c + 1])
+        nc.sync.dma_start(out=out[0 : 2 * P, :].rearrange("(c p) j -> p c j", p=P), in_=res_pair[:])
 
-        def cross(c, j0, n):
-            nc.vector.tensor_tensor(out=res[c][:, j0 : j0 + n], in0=x0[c][:].indirect(offs_of(j0, n)), in1=yb[c][:, j0 : j0 + n], op=ALU.mult)
-
-        def store(c, j0, n):
-            nc.sync.dma_start(out=out[c * P : (c + 1) * P, j0 : j0 + n], in_=res[c][:, j0 : j0 + n])
-
-        hidden(0)
-        hidden(1)
-        sums(0, 0)
-        sums(1, 0)
-        cross(1, 0, HALF)
-        sums(0, 1)
-        store(0, 0, J)
-        sums(1, 1)
-        cross(1, HALF, HALF)
-        store(1, 0, J)
-        for h in range(HALVES):
-            sums(2, h)
-            cross(2, h * HALF, HALF)
-        store(2, 0, J)
-        for h in range(HALVES):
-            sums(3, h)
-        j0 = 0
-        for n in LAST_PIECES:
-            cross(3, j0, n)
-            store(3, j0, n)
-            j0 += n
+        for c, pieces in ((2, [HALF, HALF]), (3, LAST_PIECES)):
+            j0 = 0
+            for n in pieces:
+                nc.vector.tensor_tensor(out=res[c][:, j0 : j0 + n], in0=x0[c][:].indirect(offs_of(j0, n)), in1=yb[c][:, j0 : j0 + n], op=ALU.mult)
+                j0 += n
+                if c == NT - 1:
+                    nc.sync.dma_start(out=out[c * P : (c + 1) * P, j0 - n : j0], in_=res[c][:, j0 - n : j0])
+            if c < NT - 1:
+                nc.sync.dma_start(out=out[c * P : (c + 1) * P, :], in_=res[c][:])

@@ -27,6 +27,7 @@ DN0 = J
 WB0 = J + R
 PLANE = J + R + N
 UP_PART = 256
+ROW0 = 96
 LAST_PIECES = [640, 256, 128]
 
 
@@ -34,51 +35,42 @@ def tile_list_xcross_relu_kernel(tc, tab_words, tab_scales, wb_words, wb_scales,
     nc = tc.nc
     with ExitStack() as ctx:
         keep = ctx.enter_context(tc.tile_pool(name="keep", bufs=1))
-        psum = ctx.enter_context(tc.psum_pool(name="psum", bufs=8))
+        psum = ctx.enter_context(tc.psum_pool(name="psum", bufs=1))
 
         offsets = keep.tile([P, J // 16], U16, name="offsets")
-        dn_raw = keep.tile([P, PASSES, R // 2], I32, name="dn_raw", align_bytes=256)
         tab_sc = keep.tile([P, T // 4], I32, name="tab_sc", align_bytes=256)
         dn_sc_raw = keep.tile([P, R // 4], I32, name="dn_sc_raw", align_bytes=256)
         staged = keep.tile([P, PLANE // 4], I32, name="staged", align_bytes=256)
         planes = keep.tile([P, PASSES, PLANE // 4], I32, name="planes", align_bytes=256)
+        dn_raw = keep.tile([P, PASSES, R // 2], I32, name="dn_raw", align_bytes=256)
+        dn_w = keep.tile([P, PASSES, 2 * R], U8, name="dn_w", align_bytes=64)
+        tab_w = keep.tile([P, T], I32, name="tab_w", align_bytes=256)
+        wb_w = keep.tile([P, PASSES, N // 2], I32, name="wb_w", align_bytes=256)
         b_rows = keep.tile([P, P], F32, name="b_rows", align_bytes=256)
         ident = keep.tile([P, P], F32, name="ident")
         b1 = keep.tile([P, NT], F32, name="b1")
-        dn_w = keep.tile([P, PASSES, 2 * R], U8, name="dn_w", align_bytes=64)
 
         def scale_rows(scales):
             return scales.rearrange("a q n -> q a n").bitcast(I32)
 
-        mid = ctx.enter_context(tc.tile_pool(name="mid", bufs=1))
-        zeros = mid.tile([P, 2 * P], F32, name="zeros", offset=4 * T - 4 * P)
-        nc.gpsimd.memset(zeros[:, 0:P], 0.0)
-        nc.vector.memset(tab_sc[:, 0 : T // 8], 0)
-        nc.gpsimd.memset(tab_sc[:, T // 8 : T // 4], 0)
-        nc.gpsimd.memset(dn_sc_raw[:], 0)
-        nc.sync.dma_start(out=dn_raw[:], in_=dn_words.rearrange("a p w -> p a w").bitcast(I32))
+        nc.sync.dma_start(out=tab_sc[ROW0:P, :], in_=scale_rows(tab_scales))
         nc.sync.dma_start(offsets[:], offs)
+        nc.scalar.dma_start(out=dn_sc_raw[ROW0:P, :], in_=scale_rows(dn_scales))
+        nc.scalar.dma_start(out=staged[ROW0:P, WB0 // 4 : (WB0 + N) // 4], in_=scale_rows(wb_scales))
         nc.scalar.dma_start(out=b_rows[P - NT : P, :], in_=b.rearrange("(c p) -> c p", p=P))
-        nc.sync.dma_start(out=staged[0:P:4, WB0 // 4 : (WB0 + N) // 4], in_=scale_rows(wb_scales))
-        nc.sync.dma_start(out=tab_sc[0:P:4, :], in_=scale_rows(tab_scales))
-        nc.sync.dma_start(out=dn_sc_raw[0:P:4, :], in_=scale_rows(dn_scales))
-
-        nc.vector.tensor_copy(out=b_rows[0 : P - NT, :], in_=zeros[0 : P - NT, 0:P])
-        make_identity(nc, ident[:])
-        nc.vector.memset(planes[:], 0)
-
-        wb_w = mid.tile([P, PASSES, N // 2], I32, name="wb_w", align_bytes=256, offset=4 * T)
-        tab_w = mid.tile([P, T], I32, name="tab_w", align_bytes=256, offset=0)
+        nc.sync.dma_start(out=dn_raw[:], in_=dn_words.rearrange("a p w -> p a w").bitcast(I32))
         nc.sync.dma_start(out=tab_w[:], in_=tab_words[0].rearrange("p t c -> p (t c)").bitcast(I32))
         nc.sync.dma_start(out=wb_w[:], in_=wb_words.rearrange("a p w -> p a w").bitcast(I32))
 
-        nc.vector.tensor_copy(
-            out=dn_w[:].bitcast(U16).rearrange("p a (t m) -> p a t m", t=4),
-            in_=dn_raw[:].bitcast(U16).rearrange("p a (m t) -> p a t m", t=4),
-        )
+        nc.vector.memset(tab_sc[0:ROW0, :], 0)
+        nc.vector.memset(dn_sc_raw[0:ROW0, :], 0)
+        nc.vector.memset(b_rows[0 : P - NT, :], 0.0)
+        nc.vector.memset(planes[:], 0)
+        make_identity(nc, ident[:])
+
         with tc.tile_pool(name="stage", bufs=1) as stage:
             g_sc = stage.tile([P, J], U8, name="g_sc", align_bytes=64)
-            b_cols = psum.tile([P, HALF], F32, name="bank")
+            b_cols = psum.tile([P, HALF], F32, name="bank_7")
             nc.tensor.transpose(b_cols[:, 0:P], b_rows[:], ident[:])
             nc.scalar.activation(out=b1[:], in_=b_cols[:, P - NT : P], func=ACT.Copy, bias=1.0)
 
@@ -90,16 +82,17 @@ def tile_list_xcross_relu_kernel(tc, tab_words, tab_scales, wb_words, wb_scales,
             nc.vector.tensor_copy(out=staged[:, 0 : J // 4], in_=g_sc[:].bitcast(I32))
 
         for q in (0, 2, 1, 3):
-            nc.sync.dma_start(out=planes[32 * q : 32 * q + 4, :, :], in_=staged[32 * q : 32 * q + 32 : 4, :])
+            nc.sync.dma_start(out=planes[32 * q : 32 * q + 4, :, :], in_=staged[ROW0 + 8 * q : ROW0 + 8 * q + 8, :])
+        nc.vector.tensor_copy(
+            out=dn_w[:].bitcast(U16).rearrange("p a (t m) -> p a t m", t=4),
+            in_=dn_raw[:].bitcast(U16).rearrange("p a (m t) -> p a t m", t=4),
+        )
 
         late = ctx.enter_context(tc.tile_pool(name="late", bufs=1))
-        x0_pair = late.tile([P, 2, T], F32, name="x0_pair", align_bytes=256)
-        nc.sync.dma_start(out=x0_pair[:], in_=x0T[0 : 2 * P, :].rearrange("(c p) t -> p c t", p=P))
         up_raw = late.tile([P, 4, N], F32, name="up_raw", align_bytes=256)
         nc.sync.dma_start(out=up_raw[:], in_=upw.rearrange("(p t) n -> p t n", t=4))
-        x0 = {}
-        for c in range(2, NT):
-            x0[c] = late.tile([P, T], F32, name="x0_%d" % c, align_bytes=256)
+        x0 = [late.tile([P, T], F32, name="x0_%d" % c, align_bytes=256) for c in range(NT)]
+        for c in range(NT):
             nc.sync.dma_start(out=x0[c][:], in_=x0T[c * P : (c + 1) * P, :])
 
         def offs_of(j0, n):
@@ -123,7 +116,7 @@ def tile_list_xcross_relu_kernel(tc, tab_words, tab_scales, wb_words, wb_scales,
         for h in range(HALVES):
             for j0 in range(0, HALF, CH):
                 for t0 in (0, 2):
-                    hs = psum.tile([P, 2, CH], F32, name="bank")
+                    hs = psum.tile([P, 2, CH], F32, name="bank_%d" % (4 * h + 2 * (j0 // CH) + t0 // 2))
                     for t in (t0, t0 + 1):
                         for a in range(PASSES):
                             nc.tensor.matmul_mx(
@@ -142,27 +135,6 @@ def tile_list_xcross_relu_kernel(tc, tab_words, tab_scales, wb_words, wb_scales,
                         nc.vector.tensor_scalar_max(out=pairs, in0=hs[:].rearrange("p t n -> p n t"), scalar1=0.0)
             nc.vector.quantize_mx(out=h_w[h][:].bitcast(FP8X4), scales=h_sc[h][:], in_=h_bf[h][:].rearrange("p j t -> p (j t)"))
 
-        y = {}
-        for c in range(NT):
-            for h in range(HALVES):
-                y[c, h] = psum.tile([P, HALF], F32, name="bank")
-                for a in range(PASSES):
-                    nc.tensor.matmul_mx(
-                        out=y[c, h][:],
-                        lhsT=wb_w[:, a, :].bitcast(U8)[:, 2 * P * c : 2 * P * (c + 1)].bitcast(FP4X4),
-                        lhsT_scale=plane(a, WB0 + P * c, P),
-                        rhs=t_w[h][:, a, :].bitcast(FP4X4),
-                        rhs_scale=plane(a, h * HALF, HALF),
-                        start=(a == 0),
-                        stop=False,
-                    )
-
-        g_0 = keep.tile([P, J], F32, name="h_bf_1", align_bytes=64)
-        nc.vector.tensor_copy(out=g_0[:], in_=x0_pair[:, 0, :].indirect(offsets[:]))
-        g_10 = keep.tile([P, HALF], F32, name="h_bf_0", align_bytes=64)
-        nc.vector.tensor_copy(out=g_10[:], in_=x0_pair[:, 1, :].indirect(offs_of(0, HALF)))
-        g = {(0, 0): g_0[:, 0:HALF], (0, 1): g_0[:, HALF:J], (1, 0): g_10[:]}
-
         up_w, up_sc = [], []
         for u in range(N // UP_PART):
             up_bf = keep.tile([P, UP_PART, 4], BF16, name="up_bf_%d" % u, align_bytes=64)
@@ -174,20 +146,26 @@ def tile_list_xcross_relu_kernel(tc, tab_words, tab_scales, wb_words, wb_scales,
                 func=ACT.Copy,
             )
             nc.vector.quantize_mx(out=up_w[u][:].bitcast(FP8X4), scales=up_sc[u][:], in_=up_bf[:].rearrange("p n t -> p (n t)"))
-            if u == 0:
-                g_11 = keep.tile([P, HALF], F32, name="up_bf_0", align_bytes=64)
-                nc.vector.tensor_copy(out=g_11[:], in_=x0_pair[:, 1, :].indirect(offs_of(HALF, HALF)))
-                g[1, 1] = g_11[:]
 
+        yb = [keep.tile([P, J], F32, name="yb_%d" % c) for c in range(NT)]
         res_pair = keep.tile([P, 2, J], F32, name="res_pair", align_bytes=256)
-        yb = {c: keep.tile([P, J], F32, name="yb_%d" % c) for c in range(2, NT)}
-        res = {c: keep.tile([P, J], F32, name="res_%d" % c, align_bytes=256) for c in range(2, NT)}
-        for c in range(NT):
-            u, n0 = divmod(c * P, UP_PART)
-            for h in range(HALVES):
-                cols = slice(h * HALF, (h + 1) * HALF)
+        res = [res_pair[:, 0, :], res_pair[:, 1, :]] + [keep.tile([P, J], F32, name="res_%d" % c, align_bytes=256)[:] for c in range(2, NT)]
+        for c0 in range(0, NT, 2):
+            for h, c in [(h, c) for h in range(HALVES) for c in (c0, c0 + 1)]:
+                u, n0 = divmod(c * P, UP_PART)
+                y = psum.tile([P, HALF], F32, name="bank_%d" % (2 * h + c - c0))
+                for a in range(PASSES):
+                    nc.tensor.matmul_mx(
+                        out=y[:],
+                        lhsT=wb_w[:, a, :].bitcast(U8)[:, 2 * P * c : 2 * P * (c + 1)].bitcast(FP4X4),
+                        lhsT_scale=plane(a, WB0 + P * c, P),
+                        rhs=t_w[h][:, a, :].bitcast(FP4X4),
+                        rhs_scale=plane(a, h * HALF, HALF),
+                        start=(a == 0),
+                        stop=False,
+                    )
                 nc.tensor.matmul_mx(
-                    out=y[c, h][:],
+                    out=y[:],
                     lhsT=up_w[u][:, n0 : n0 + P].bitcast(FP8X4),
                     lhsT_scale=up_sc[u][:, n0 : n0 + P],
                     rhs=h_w[h][:].bitcast(FP8X4),
@@ -195,20 +173,17 @@ def tile_list_xcross_relu_kernel(tc, tab_words, tab_scales, wb_words, wb_scales,
                     start=False,
                     stop=True,
                 )
-                if c < 2:
-                    nc.vector.scalar_tensor_tensor(
-                        out=res_pair[:, c, cols], in0=y[c, h][:], scalar=b1[:, c : c + 1], in1=g[c, h], op0=ALU.add, op1=ALU.mult
-                    )
-                else:
-                    nc.scalar.activation(out=yb[c][:, cols], in_=y[c, h][:], func=ACT.Identity, bias=b1[:, c : c + 1])
-        nc.sync.dma_start(out=out[0 : 2 * P, :].rearrange("(c p) j -> p c j", p=P), in_=res_pair[:])
+                nc.scalar.activation(out=yb[c][:, h * HALF : (h + 1) * HALF], in_=y[:], func=ACT.Identity, bias=b1[:, c : c + 1])
 
-        for c, pieces in ((2, [HALF, HALF]), (3, LAST_PIECES)):
+        for c in range(NT):
+            last = c == NT - 1
             j0 = 0
-            for n in pieces:
+            for n in LAST_PIECES if last else [HALF] * HALVES:
                 nc.vector.tensor_tensor(out=res[c][:, j0 : j0 + n], in0=x0[c][:].indirect(offs_of(j0, n)), in1=yb[c][:, j0 : j0 + n], op=ALU.mult)
+                if last:
+                    nc.sync.dma_start(out=out[c * P : (c + 1) * P, j0 : j0 + n], in_=res[c][:, j0 : j0 + n])
                 j0 += n
-                if c == NT - 1:
-                    nc.sync.dma_start(out=out[c * P : (c + 1) * P, j0 - n : j0], in_=res[c][:, j0 - n : j0])
-            if c < NT - 1:
-                nc.sync.dma_start(out=out[c * P : (c + 1) * P, :], in_=res[c][:])
+            if c == 1:
+                nc.sync.dma_start(out=out[0 : 2 * P, :].rearrange("(c p) j -> p c j", p=P), in_=res_pair[:])
+            if c == 2:
+                nc.sync.dma_start(out=out[c * P : (c + 1) * P, :], in_=res[c])

@@ -148,8 +148,7 @@ def tile_list_xcross_relu_kernel(tc, tab_words, tab_scales, wb_words, wb_scales,
             nc.vector.quantize_mx(out=up_w[u][:].bitcast(FP8X4), scales=up_sc[u][:], in_=up_bf[:].rearrange("p n t -> p (n t)"))
 
         yb = [keep.tile([P, J], F32, name="yb_%d" % c) for c in range(NT)]
-        res_pair = keep.tile([P, 2, J], F32, name="res_pair", align_bytes=256)
-        res = [res_pair[:, 0, :], res_pair[:, 1, :]] + [keep.tile([P, J], F32, name="res_%d" % c, align_bytes=256)[:] for c in range(2, NT)]
+        res = [keep.tile([P, J], F32, name="res_%d" % c, align_bytes=256) for c in range(NT)]
         for c0 in range(0, NT, 2):
             for h, c in [(h, c) for h in range(HALVES) for c in (c0, c0 + 1)]:
                 u, n0 = divmod(c * P, UP_PART)
@@ -183,7 +182,5 @@ def tile_list_xcross_relu_kernel(tc, tab_words, tab_scales, wb_words, wb_scales,
                 if last:
                     nc.sync.dma_start(out=out[c * P : (c + 1) * P, j0 : j0 + n], in_=res[c][:, j0 : j0 + n])
                 j0 += n
-            if c == 1:
-                nc.sync.dma_start(out=out[0 : 2 * P, :].rearrange("(c p) j -> p c j", p=P), in_=res_pair[:])
-            if c == 2:
-                nc.sync.dma_start(out=out[c * P : (c + 1) * P, :], in_=res[c])
+            if not last:
+                nc.sync.dma_start(out=out[c * P : (c + 1) * P, :], in_=res[c][:])

from contextlib import ExitStack

import concourse.mybir as mybir
from concourse.masks import make_identity

K, R, N, T, J = 1024, 512, 512, 4096, 1024
FLOPS = 2 * J * (K * R + K * N + R * N)

F32 = mybir.dt.float32
BF16 = mybir.dt.bfloat16
I32 = mybir.dt.int32
U32 = mybir.dt.uint32
U16 = mybir.dt.uint16
U8 = mybir.dt.uint8
FP8X4 = mybir.dt.float8_e4m3fn_x4
FP4X4 = mybir.dt.float4_e2m1fn_x4
ACT = mybir.ActivationFunctionType
ALU = mybir.AluOpType

P = 128
PASSES = 2
HALF = 512
HALVES = J // HALF
CH = 256
NT = N // P
DN0 = J
WB0 = J + R
PLANE = J + R + N
UP_PART = 256
ROW0 = 96
LAST_PIECES = [640, 256, 128]


def tile_list_xcross_relu_kernel(tc, tab_words, tab_scales, wb_words, wb_scales, dn_words, dn_scales, upw, x0T, b, offs, out):
    nc = tc.nc
    with ExitStack() as ctx:
        keep = ctx.enter_context(tc.tile_pool(name="keep", bufs=1))
        psum = ctx.enter_context(tc.psum_pool(name="psum", bufs=1))

        offsets = keep.tile([P, J // 16], U16, name="offsets")
        tab_sc = keep.tile([P, T // 4], I32, name="tab_sc", align_bytes=256)
        dn_sc_raw = keep.tile([P, R // 4], I32, name="dn_sc_raw", align_bytes=256)
        staged = keep.tile([P, PLANE // 4], I32, name="staged", align_bytes=256)
        planes = keep.tile([P, PASSES, PLANE // 4], I32, name="planes", align_bytes=256)
        dn_raw = keep.tile([P, PASSES, R // 2], I32, name="dn_raw", align_bytes=256)
        dn_w = keep.tile([P, PASSES, 2 * R], U8, name="dn_w", align_bytes=64)
        tab_w = keep.tile([P, T], I32, name="tab_w", align_bytes=256)
        wb_w = keep.tile([P, PASSES, N // 2], I32, name="wb_w", align_bytes=256)
        b_rows = keep.tile([P, P], F32, name="b_rows", align_bytes=256)
        ident = keep.tile([P, P], F32, name="ident")
        b1 = keep.tile([P, NT], F32, name="b1")

        def scale_rows(scales):
            return scales.rearrange("a q n -> q a n").bitcast(I32)

        nc.sync.dma_start(out=tab_sc[ROW0:P, :], in_=scale_rows(tab_scales))
        nc.sync.dma_start(offsets[:], offs)
        nc.scalar.dma_start(out=dn_sc_raw[ROW0:P, :], in_=scale_rows(dn_scales))
        nc.scalar.dma_start(out=staged[ROW0:P, WB0 // 4 : (WB0 + N) // 4], in_=scale_rows(wb_scales))
        nc.scalar.dma_start(out=b_rows[P - NT : P, :], in_=b.rearrange("(c p) -> c p", p=P))
        nc.sync.dma_start(out=dn_raw[:], in_=dn_words.rearrange("a p w -> p a w").bitcast(I32))
        nc.sync.dma_start(out=tab_w[:], in_=tab_words[0].rearrange("p t c -> p (t c)").bitcast(I32))
        nc.sync.dma_start(out=wb_w[:], in_=wb_words.rearrange("a p w -> p a w").bitcast(I32))

        nc.vector.memset(tab_sc[0:ROW0, :], 0)
        nc.vector.memset(dn_sc_raw[0:ROW0, :], 0)
        nc.vector.memset(b_rows[0 : P - NT, :], 0.0)
        nc.vector.memset(planes[:], 0)
        make_identity(nc, ident[:])

        with tc.tile_pool(name="stage", bufs=1) as stage:
            g_sc = stage.tile([P, J], U8, name="g_sc", align_bytes=64)
            b_cols = psum.tile([P, HALF], F32, name="bank_7")
            nc.tensor.transpose(b_cols[:, 0:P], b_rows[:], ident[:])
            nc.scalar.activation(out=b1[:], in_=b_cols[:, P - NT : P], func=ACT.Copy, bias=1.0)

            nc.vector.tensor_copy(out=g_sc[:], in_=tab_sc[:].bitcast(U8).indirect(offsets[:]))
            nc.vector.tensor_copy(
                out=staged[:].bitcast(U8)[:, DN0 : DN0 + R].rearrange("p (t m) -> p t m", t=4),
                in_=dn_sc_raw[:].bitcast(U8).rearrange("p (m t) -> p t m", t=4),
            )
            nc.vector.tensor_copy(out=staged[:, 0 : J // 4], in_=g_sc[:].bitcast(I32))

        for q in (0, 2, 1, 3):
            nc.sync.dma_start(out=planes[32 * q : 32 * q + 4, :, :], in_=staged[ROW0 + 8 * q : ROW0 + 8 * q + 8, :])
        nc.vector.tensor_copy(
            out=dn_w[:].bitcast(U16).rearrange("p a (t m) -> p a t m", t=4),
            in_=dn_raw[:].bitcast(U16).rearrange("p a (m t) -> p a t m", t=4),
        )

        late = ctx.enter_context(tc.tile_pool(name="late", bufs=1))
        up_raw = late.tile([P, 4, N], F32, name="up_raw", align_bytes=256)
        nc.sync.dma_start(out=up_raw[:], in_=upw.rearrange("(p t) n -> p t n", t=4))
        x0 = [late.tile([P, T], F32, name="x0_%d" % c, align_bytes=256) for c in range(NT)]
        for c in range(NT):
            nc.sync.dma_start(out=x0[c][:], in_=x0T[c * P : (c + 1) * P, :])

        def offs_of(j0, n):
            return offsets[:, j0 // 16 : (j0 + n) // 16]

        def plane(a, c0, n):
            return planes[:, a, :].bitcast(U8)[:, c0 : c0 + n]

        t_w = [keep.tile([P, PASSES, 2 * HALF], U8, name="t_w_%d" % h, align_bytes=64) for h in range(HALVES)]
        for h in range(HALVES):
            g_w = late.tile([P, HALF], U32, name="g_w", align_bytes=64)
            nc.vector.tensor_copy(out=g_w[:], in_=tab_w[:].bitcast(U32).indirect(offs_of(h * HALF, HALF)))
            nc.vector.tensor_copy(
                out=t_w[h][:].bitcast(U16),
                in_=g_w[:].bitcast(U16).rearrange("p (j d) -> p d j", d=PASSES),
            )

        h_bf = [keep.tile([P, HALF, 4], BF16, name="h_bf_%d" % h, align_bytes=64) for h in range(HALVES)]
        h_w = [keep.tile([P, HALF], U32, name="h_w_%d" % h, align_bytes=64) for h in range(HALVES)]
        h_sc = [keep.tile([P, HALF], U8, name="h_sc_%d" % h, align_bytes=64) for h in range(HALVES)]
        for h in range(HALVES):
            for j0 in range(0, HALF, CH):
                for t0 in (0, 2):
                    hs = psum.tile([P, 2, CH], F32, name="bank_%d" % (4 * h + 2 * (j0 // CH) + t0 // 2))
                    for t in (t0, t0 + 1):
                        for a in range(PASSES):
                            nc.tensor.matmul_mx(
                                out=hs[:, t - t0, :],
                                lhsT=dn_w[:, a, 2 * P * t : 2 * P * (t + 1)].bitcast(FP4X4),
                                lhsT_scale=plane(a, DN0 + P * t, P),
                                rhs=t_w[h][:, a, 2 * j0 : 2 * (j0 + CH)].bitcast(FP4X4),
                                rhs_scale=plane(a, h * HALF + j0, CH),
                                start=(a == 0),
                                stop=(a == PASSES - 1),
                            )
                    pairs = h_bf[h][:, j0 : j0 + CH, t0 : t0 + 2]
                    if t0 == 0:
                        nc.scalar.activation(out=pairs, in_=hs[:].rearrange("p t n -> p n t"), func=ACT.Relu)
                    else:
                        nc.vector.tensor_scalar_max(out=pairs, in0=hs[:].rearrange("p t n -> p n t"), scalar1=0.0)
            nc.vector.quantize_mx(out=h_w[h][:].bitcast(FP8X4), scales=h_sc[h][:], in_=h_bf[h][:].rearrange("p j t -> p (j t)"))

        up_w, up_sc = [], []
        for u in range(N // UP_PART):
            up_bf = keep.tile([P, UP_PART, 4], BF16, name="up_bf_%d" % u, align_bytes=64)
            up_w.append(keep.tile([P, UP_PART], U32, name="up_w_%d" % u, align_bytes=64))
            up_sc.append(keep.tile([P, UP_PART], U8, name="up_sc_%d" % u, align_bytes=64))
            nc.scalar.activation(
                out=up_bf[:].rearrange("p (c i) t -> p c t i", i=4),
                in_=up_raw[:, :, u * UP_PART : (u + 1) * UP_PART].rearrange("p t (c i) -> p c t i", i=4),
                func=ACT.Copy,
            )
            nc.vector.quantize_mx(out=up_w[u][:].bitcast(FP8X4), scales=up_sc[u][:], in_=up_bf[:].rearrange("p n t -> p (n t)"))

        yb = [keep.tile([P, J], F32, name="yb_%d" % c) for c in range(NT)]
        res = [keep.tile([P, J], F32, name="res_%d" % c, align_bytes=256) for c in range(NT)]
        for c0 in range(0, NT, 2):
            for h, c in [(h, c) for h in range(HALVES) for c in (c0, c0 + 1)]:
                u, n0 = divmod(c * P, UP_PART)
                y = psum.tile([P, HALF], F32, name="bank_%d" % (2 * h + c - c0))
                for a in range(PASSES):
                    nc.tensor.matmul_mx(
                        out=y[:],
                        lhsT=wb_w[:, a, :].bitcast(U8)[:, 2 * P * c : 2 * P * (c + 1)].bitcast(FP4X4),
                        lhsT_scale=plane(a, WB0 + P * c, P),
                        rhs=t_w[h][:, a, :].bitcast(FP4X4),
                        rhs_scale=plane(a, h * HALF, HALF),
                        start=(a == 0),
                        stop=False,
                    )
                nc.tensor.matmul_mx(
                    out=y[:],
                    lhsT=up_w[u][:, n0 : n0 + P].bitcast(FP8X4),
                    lhsT_scale=up_sc[u][:, n0 : n0 + P],
                    rhs=h_w[h][:].bitcast(FP8X4),
                    rhs_scale=h_sc[h][:],
                    start=False,
                    stop=True,
                )
                nc.scalar.activation(out=yb[c][:, h * HALF : (h + 1) * HALF], in_=y[:], func=ACT.Identity, bias=b1[:, c : c + 1])

        for c in range(NT):
            last = c == NT - 1
            j0 = 0
            for n in LAST_PIECES if last else [HALF] * HALVES:
                nc.vector.tensor_tensor(out=res[c][:, j0 : j0 + n], in0=x0[c][:].indirect(offs_of(j0, n)), in1=yb[c][:, j0 : j0 + n], op=ALU.mult)
                if last:
                    nc.sync.dma_start(out=out[c * P : (c + 1) * P, j0 : j0 + n], in_=res[c][:, j0 : j0 + n])
                j0 += n
            if not last:
                nc.sync.dma_start(out=out[c * P : (c + 1) * P, :], in_=res[c][:])
